import numpy as np
import ml_dtypes


def mxq(x, axis, fmt="e4m3"):
    dtype, down = {"e4m3": (ml_dtypes.float8_e4m3fn, 7), "e5m2": (ml_dtypes.float8_e5m2, 14)}[fmt]
    v = np.moveaxis(np.asarray(x, np.float32).astype(ml_dtypes.bfloat16).astype(np.float64), axis, -1)
    blocks = v.reshape(v.shape[:-1] + (-1, 32))
    amax = np.abs(blocks).max(-1, keepdims=True)
    byte = np.maximum(np.where(amax > 0, np.frexp(amax)[1] - 1 + 127, 0) - down, 1)
    scale = np.exp2(byte - 127.0)
    codes = (blocks / scale).astype(np.float32).astype(dtype).astype(np.float64)
    return np.moveaxis((codes * scale).reshape(v.shape), -1, axis)


WIDE = False


def mx_kscale(k):
    if not WIDE:
        return np.ones(k)
    levels = np.array([10, -10, 5, -5, 0])
    if k % 512:
        return np.exp2(np.random.permutation(np.resize(levels, k // 32))).repeat(32)
    a = np.empty((k // 512, 16))
    for p in range(k // 512):
        a[p, :8] = np.random.permutation(np.resize(levels, 8))
        for g in range(8):
            far = levels[np.abs(levels - a[p, g]) >= 10]
            a[p, g + 8] = far[np.random.randint(len(far))]
    return np.exp2(a.ravel()).repeat(32)


BF16 = ml_dtypes.bfloat16


def bf(x):
    return np.asarray(x, np.float32).astype(BF16)


def f64(x):
    return np.asarray(x).astype(np.float64)


DI, R, DO, S = 1024, 512, 1024, 1024


def draw0():
    sr = mx_kscale(R)
    ss = mx_kscale(S)
    t = mx_kscale(DO)
    m = np.random.standard_normal((DI, R)) * sr[None, :]
    a_old = np.random.standard_normal((R, DO)) / np.sqrt(R) / sr[:, None] * t[None, :]
    a_new = np.random.standard_normal((R, DO)) / np.sqrt(DO) / t[None, :]
    x = np.random.standard_normal((S, DI)) * ss[:, None]
    dy = np.random.standard_normal((S, DO)) / ss[:, None] * t[None, :]
    return {"m": bf(m), "a_old": bf(a_old), "a_new": bf(a_new), "x": bf(x), "dy": bf(dy)}


def weight_gradient(x, dy):
    tokens = x.shape[0]
    return (mxq(x.T, 1, "e4m3") @ mxq(dy, 0, "e4m3")) / np.sqrt(tokens)


def row_rms_normalise(v):
    mean_sq = np.mean(v * v, axis=-1, keepdims=True)
    return v / np.sqrt(mean_sq + 0.1)


def core(m, a_old, a_new, x, dy):
    d = mxq(f64(m), 1, "e4m3") @ mxq(f64(a_old), 0, "e4m3")
    g = weight_gradient(f64(x), f64(dy))
    h = 0.8 * d + 0.6 * g
    mn = mxq(h, 1, "e4m3") @ mxq(f64(a_new).T, 0, "e4m3")
    return row_rms_normalise(mn)


def e4m3fn_bytes(y):
    return np.clip(np.asarray(y, np.float64), -448.0, 448.0).astype(np.float32).astype(ml_dtypes.float8_e4m3fn).view(np.uint8)


def e4m3fn_values(b):
    return np.asarray(b, np.uint8).view(ml_dtypes.float8_e4m3fn).astype(np.float64)


def setup_inputs():
    d = draw0()
    x0 = np.asarray(d['x']).astype(np.float64)
    s = (np.max(np.abs(x0), axis=(1,), keepdims=True) / 448.0).astype(np.float32)
    out = {}
    for k, v in d.items():
        if k == 'x':
            out['x_bytes'] = e4m3fn_bytes(x0 / s.astype(np.float64))
            out['x_scale'] = s
        else:
            out[k] = v
    return out


def reference(m, a_old, a_new, x_bytes, x_scale, dy):
    return core(m, a_old, a_new, e4m3fn_values(x_bytes) * x_scale.astype(np.float64), dy)

@@ -1,0 +1,450 @@
+from contextlib import ExitStack
+
+import concourse.mybir as mybir
+from concourse.masks import make_identity
+
+DI, R, DO, S = 1024, 512, 1024, 1024
+
+F32 = mybir.dt.float32
+BF16 = mybir.dt.bfloat16
+U32 = mybir.dt.uint32
+U8 = mybir.dt.uint8
+FP8 = mybir.dt.float8_e4m3fn
+FP8X4 = mybir.dt.float8_e4m3fn_x4
+ACT = mybir.ActivationFunctionType
+ALU = mybir.AluOpType
+
+FLOPS = 2 * (DI * R * DO + DI * S * DO + DI * DO * R)
+
+P = 128
+PACK = 4
+KP = P * PACK
+NB = DI // P
+HC = 512
+XC = ((0, 256), (256, 256), (512, 512))
+
+
+def tile_floramomentumsubspacetransfer_kernel(tc, m, a_old, a_new, x_bytes, x_scale, dy, out):
+    nc = tc.nc
+    with ExitStack() as ctx:
+        keep = ctx.enter_context(tc.tile_pool(name="keep", bufs=1))
+        wide = ctx.enter_context(tc.tile_pool(name="wide", bufs=4))
+        group = ctx.enter_context(tc.tile_pool(name="group", bufs=10))
+        work = ctx.enter_context(tc.tile_pool(name="work", bufs=3))
+        psum = ctx.enter_context(tc.psum_pool(name="psum", bufs=2))
+
+        ident = keep.tile([P, P], F32, name="ident")
+        identb = keep.tile([P, P], BF16, name="identb")
+        eps = keep.tile([P, 1], F32, name="eps")
+        warm = keep.tile([P, 1], F32, name="warm")
+        xsc = keep.tile([P, 2, PACK], F32, name="xsc")
+        xb = [keep.tile([P, PACK, DI], U8, name="xb%d" % p) for p in range(2)]
+        dyr = {(p, g): keep.tile([P, PACK, HC], BF16, name="dyr%d%d" % (p, g)) for p in range(2) for g in range(2)}
+        aor = [keep.tile([P, PACK, HC], BF16, name="aor%d" % g) for g in range(2)]
+        mr = [keep.tile([P, 4, R], BF16, name="mr%d" % h) for h in range(2)]
+        anr = keep.tile([P, 4, DO], BF16, name="anr")
+
+        def operand(name, width):
+            return (keep.tile([P, width], U32, align_bytes=64, name=name + "c"), keep.tile([P, width], U8, align_bytes=64, name=name + "s"))
+
+        xq = {(p, c): operand("xq%d%d" % (p, c), XC[c][1]) for p in range(2) for c in range(len(XC))}
+        dq = {(p, g): operand("dq%d%d" % (p, g), HC) for p in range(2) for g in range(2)}
+        aq = [operand("aq%d" % g, HC) for g in range(2)]
+        mq = {(h, k): operand("mq%d%d" % (h, k), 256) for h in range(2) for k in range(2)}
+        nq = [operand("nq%d" % p, R) for p in range(2)]
+        hq = {}
+
+        nc.sync.dma_start(out=xsc[:], in_=x_scale.rearrange("(g p t) o -> p g (t o)", p=P, t=PACK))
+        for p in range(2):
+            nc.sync.dma_start(out=xb[p][:], in_=x_bytes.rearrange("(g p t) n -> g p t n", p=P, t=PACK)[p])
+
+        def load_dy(p, g):
+            nc.sync.dma_start(out=dyr[p, g][:], in_=dy.rearrange("(q p t) n -> q p t n", p=P, t=PACK)[p][:, :, g * HC : (g + 1) * HC])
+
+        def load_ao(g):
+            nc.sync.dma_start(out=aor[g][:], in_=a_old.rearrange("(p t) n -> p t n", t=PACK)[:, :, g * HC : (g + 1) * HC])
+
+        def load_m(h):
+            nc.sync.dma_start(out=mr[h][:], in_=m.rearrange("(h i p) k -> h p i k", p=P, i=4)[h])
+
+        load_m(1)
+        load_ao(1)
+        load_ao(0)
+        load_m(0)
+        load_dy(0, 0)
+        load_dy(1, 0)
+        load_dy(1, 1)
+        nc.sync.dma_start(out=anr[:], in_=a_new.rearrange("(i p) k -> p i k", p=P))
+        load_dy(0, 1)
+
+        make_identity(nc, ident[:])
+        make_identity(nc, identb[:])
+        nc.vector.memset(warm[:], 1.0)
+        nc.vector.memset(eps[:], 0.0)
+        nc.vector.tensor_scalar(out=eps[:], in0=eps[:], scalar1=0.1, scalar2=None, op0=ALU.add)
+        nc.scalar.activation(out=warm[:], in_=warm[:], func=ACT.Abs_reciprocal_sqrt, scale=1.0)
+
+        xw, xg, dg, ag, mg, ng = {}, {}, {}, {}, {}, {}
+        tr, pd, pg, dsb, hb, pm, ssq, rst, res = {}, {}, {}, {}, {}, {}, {}, {}, {}
+
+        def q(opnd, tile):
+            nc.vector.quantize_mx(out=opnd[0].bitcast(FP8X4), scales=opnd[1], in_=tile)
+
+        def XW(eng, p, c, j):
+            c0, w = XC[c]
+            if (p, c) not in xw:
+                xw[p, c] = wide.tile([P, PACK, w], BF16, name="xw%d" % w, bufs=1024 // w)
+            src = xb[p][:, j, c0 : c0 + w].bitcast(FP8)
+            dst = xw[p, c][:, j, :]
+            if eng == "S":
+                nc.scalar.activation(out=dst, in_=src, func=ACT.Copy, scale=xsc[:, p, j : j + 1])
+            else:
+                nc.vector.tensor_scalar(out=dst, in0=src, scalar1=xsc[:, p, j : j + 1], scalar2=None, op0=ALU.mult)
+
+        def copy(eng, dst, src):
+            if eng == "S":
+                nc.scalar.copy(out=dst, in_=src)
+            else:
+                nc.vector.tensor_copy(out=dst, in_=src)
+
+        def XI(eng, p, c):
+            xg[p, c] = group.tile([P, XC[c][1], PACK], BF16, align_bytes=64, name="xg%d" % XC[c][1], bufs=1024 // XC[c][1])
+            copy(eng, xg[p, c][:], xw[p, c][:].rearrange("p j c -> p c j"))
+
+        def XQ(p, c):
+            q((xq[p, c][0][:], xq[p, c][1][:]), xg[p, c][:].rearrange("p c j -> p (c j)"))
+
+        def perm(eng, dst, src):
+            copy(eng, dst[:].rearrange("p (t m) j -> p t m j", t=PACK), src[:].rearrange("p j (m t) -> p t m j", t=PACK))
+
+        def DG(eng, p, g):
+            dg[p, g] = group.tile([P, HC, PACK], BF16, align_bytes=64, name="grp")
+            perm(eng, dg[p, g], dyr[p, g])
+
+        def II(src, k):
+            bank = psum.tile([P, 2, P, PACK], BF16, name="tr")
+            for t in range(2):
+                nc.tensor.matmul(bank[:, t, :, :], identb[:], src[:, :, 2 * k + t :: 4].rearrange("p j m -> p m j"), start=True, stop=True)
+            return bank
+
+        def IC(eng, dst, bank, k):
+            copy(eng, dst[:, 256 * k : 256 * (k + 1), :], bank[:].rearrange("p t m j -> p (t m) j"))
+
+        def DI_(p, g, k):
+            tr["d", p, g, k] = II(dyr[p, g], k)
+
+        def DC(eng, p, g, k):
+            if (p, g) not in dg:
+                dg[p, g] = group.tile([P, HC, PACK], BF16, align_bytes=64, name="grp")
+            IC(eng, dg[p, g], tr["d", p, g, k], k)
+
+        def AI(g, k):
+            tr["a", g, k] = II(aor[g], k)
+
+        def AC(eng, g, k):
+            if g not in ag:
+                ag[g] = group.tile([P, HC, PACK], BF16, align_bytes=64, name="grp")
+            IC(eng, ag[g], tr["a", g, k], k)
+
+        def DQ(p, g):
+            q((dq[p, g][0][:], dq[p, g][1][:]), dg[p, g][:].rearrange("p c j -> p (c j)"))
+
+        def AG(eng, g):
+            ag[g] = group.tile([P, HC, PACK], BF16, align_bytes=64, name="grp")
+            perm(eng, ag[g], aor[g])
+
+        def AQ(g):
+            q((aq[g][0][:], aq[g][1][:]), ag[g][:].rearrange("p c j -> p (c j)"))
+
+        def transposes(bank, rows, first_word):
+            for i in range(2):
+                for u in range(2):
+                    nc.tensor.transpose(bank[:, i, u, :], rows[i][:, first_word + u : first_word + 256 : 2], ident[:])
+
+        def MT(h, k):
+            tr["m", h, k] = psum.tile([P, 2, 2, P], F32, name="tr")
+            transposes(tr["m", h, k], [mr[h][:, 2 * k + i, :].bitcast(F32) for i in range(2)], 0)
+
+        def MC(eng, h, k):
+            if h not in mg:
+                mg[h] = group.tile([P, HC, PACK], BF16, align_bytes=64, name="grp")
+            dst = mg[h][:, 256 * k : 256 * (k + 1), :].rearrange("p c j -> p (c j)").bitcast(F32).rearrange("p (i r u) -> p i r u", i=2, u=2)
+            copy(eng, dst, tr["m", h, k][:].rearrange("p i u r -> p i r u"))
+
+        def MQ(h, k):
+            q((mq[h, k][0][:], mq[h, k][1][:]), mg[h][:, 256 * k : 256 * (k + 1), :].rearrange("p c j -> p (c j)"))
+
+        def NT(p, k):
+            tr["n", p, k] = psum.tile([P, 2, 2, P], F32, name="tr")
+            transposes(tr["n", p, k], [anr[:, 2 * k + i, :].bitcast(F32) for i in range(2)], 256 * p)
+
+        def NC(eng, p, k):
+            if p not in ng:
+                ng[p] = group.tile([P, R, PACK], BF16, align_bytes=64, name="grp")
+            dst = ng[p][:, 256 * k : 256 * (k + 1), :].rearrange("p c j -> p (c j)").bitcast(F32).rearrange("p (i r u) -> p i r u", i=2, u=2)
+            copy(eng, dst, tr["n", p, k][:].rearrange("p i u r -> p i r u"))
+
+        def NQ(p):
+            q((nq[p][0][:], nq[p][1][:]), ng[p][:].rearrange("p c j -> p (c j)"))
+
+        def mm(dst, w, wc, mov, mc, start, stop):
+            nc.tensor.matmul_mx(
+                out=dst,
+                lhsT=w[0][:, wc].bitcast(FP8X4),
+                lhsT_scale=w[1][:, wc],
+                rhs=mov[0][:, mc].bitcast(FP8X4),
+                rhs_scale=mov[1][:, mc],
+                start=start,
+                stop=stop,
+            )
+
+        def PG(g, i):
+            pg[g, i] = psum.tile([P, PACK, P], F32, name="acc", bufs=6)
+            c = max(c for c in range(len(XC)) if XC[c][0] <= P * i)
+            cols = slice(P * i - XC[c][0], P * i - XC[c][0] + P)
+            for t in range(PACK):
+                for p in range(2):
+                    mm(pg[g, i][:, t, :], dq[p, g], slice(P * t, P * t + P), xq[p, c], cols, p == 0, p == 1)
+
+        def PD(g, i):
+            pd[g, i] = psum.tile([P, PACK, P], F32, name="acc", bufs=6)
+            k, c = divmod(i, 2)
+            for t in range(PACK):
+                mm(pd[g, i][:, t, :], aq[g], slice(P * t, P * t + P), mq[k // 2, k % 2], slice(P * c, P * c + P), True, True)
+
+        def SD(g, i):
+            dsb[g, i] = work.tile([P, P, PACK], F32, name="dsb", bufs=16)
+            nc.scalar.activation(out=dsb[g, i][:], in_=pd[g, i][:].rearrange("p t n -> p n t"), func=ACT.Copy, scale=0.8)
+
+        def VH(g, i):
+            hb[g, i] = work.tile([P, P, PACK], BF16, align_bytes=64, name="hb", bufs=14)
+            nc.vector.scalar_tensor_tensor(out=hb[g, i][:], in0=pg[g, i][:].rearrange("p t n -> p n t"), scalar=0.6 / 32.0, in1=dsb[g, i][:], op0=ALU.mult, op1=ALU.add)
+
+        def HQ(g, i):
+            hq[g, i] = operand("h%d%d" % (g, i), P)
+            q((hq[g, i][0][:], hq[g, i][1][:]), hb[g, i][:].rearrange("p n t -> p (n t)"))
+
+        def PM(i):
+            pm[i] = psum.tile([P, R], F32, name="acc", bufs=6)
+            for g in range(2):
+                mm(pm[i][:], hq[g, i], slice(0, P), nq[g], slice(0, R), g == 0, g == 1)
+
+        def SS(i):
+            ssq[i] = work.tile([P, 1], F32, name="ssq", bufs=8)
+            rst[i] = work.tile([P, 1], F32, name="rst", bufs=8)
+            junk = work.tile([P, R], BF16, name="junk", bufs=2)
+            nc.scalar.activation(out=junk[:], in_=pm[i][:], func=ACT.Square, accum_out=ssq[i][:])
+
+        def RS(i):
+            nc.scalar.activation(out=rst[i][:], in_=ssq[i][:], func=ACT.Abs_reciprocal_sqrt, scale=1.0 / R, bias=eps[:])
+
+        def FS(eng, i):
+            res[i] = work.tile([P, R], F32, name="res", bufs=6)
+            if eng == "S":
+                nc.scalar.activation(out=res[i][:], in_=pm[i][:], func=ACT.Copy, scale=rst[i][:])
+            else:
+                nc.vector.tensor_scalar(out=res[i][:], in0=pm[i][:], scalar1=rst[i][:], scalar2=None, op0=ALU.mult)
+
+        def ST(i):
+            nc.sync.dma_start(out=out[P * i : P * (i + 1), :], in_=res[i][:])
+
+        with tc.manual_schedule():
+            XW("V", 0, 1, 0)
+            XW("V", 0, 0, 0)
+            XW("V", 0, 2, 3)
+            XW("V", 0, 2, 1)
+            XW("V", 0, 1, 3)
+            XW("S", 0, 2, 0)
+            XW("V", 0, 0, 2)
+            XW("S", 0, 2, 2)
+            MT(1, 1)
+            MT(1, 0)
+            XW("S", 0, 0, 1)
+            XI("V", 0, 2)
+            XW("S", 0, 0, 3)
+            XW("S", 0, 1, 1)
+            AG("V", 1)
+            MC("S", 1, 1)
+            AI(0, 1)
+            MC("S", 1, 0)
+            AI(0, 0)
+            XI("S", 0, 0)
+            MQ(1, 0)
+            AQ(1)
+            MQ(1, 1)
+            XW("S", 0, 1, 2)
+            AC("S", 0, 1)
+            XQ(0, 2)
+            XQ(0, 0)
+            AC("S", 0, 0)
+            PD(1, 4)
+            AQ(0)
+            PD(1, 6)
+            XW("V", 1, 0, 2)
+            XW("V", 1, 2, 2)
+            MT(0, 0)
+            MT(0, 1)
+            SD(1, 4)
+            XW("S", 1, 0, 1)
+            MC("S", 0, 0)
+            SD(1, 6)
+            XW("V", 1, 2, 0)
+            XW("V", 1, 1, 1)
+            XW("V", 1, 1, 2)
+            MC("S", 0, 1)
+            PD(0, 6)
+            SD(0, 6)
+            XW("V", 1, 0, 0)
+            MQ(0, 0)
+            XW("V", 1, 2, 3)
+            PD(0, 5)
+            XW("V", 1, 2, 1)
+            XW("V", 1, 0, 3)
+            XW("V", 1, 1, 3)
+            XI("V", 1, 2)
+            DI_(0, 0, 1)
+            MQ(0, 1)
+            PD(1, 5)
+            DI_(0, 0, 0)
+            DC("S", 0, 0, 1)
+            PD(0, 4)
+            PD(1, 1)
+            DC("S", 0, 0, 0)
+            SD(1, 5)
+            SD(0, 5)
+            PD(0, 7)
+            SD(0, 4)
+            DI_(1, 0, 0)
+            DI_(1, 0, 1)
+            PD(0, 3)
+            DC("S", 1, 0, 0)
+            DC("S", 1, 0, 1)
+            SD(1, 1)
+            XQ(1, 2)
+            PD(0, 0)
+            PD(1, 0)
+            DQ(0, 0)
+            DG("V", 1, 1)
+            PD(1, 7)
+            DQ(1, 0)
+            SD(0, 7)
+            SD(0, 3)
+            NT(1, 1)
+            DQ(1, 1)
+            NT(1, 0)
+            PG(0, 4)
+            DG("V", 0, 1)
+            PG(0, 7)
+            PG(0, 6)
+            VH(0, 7)
+            SD(0, 0)
+            PG(0, 5)
+            XW("V", 1, 1, 0)
+            DQ(0, 1)
+            VH(0, 4)
+            SD(1, 0)
+            NC("S", 1, 1)
+            NC("S", 1, 0)
+            PD(0, 1)
+            SD(1, 7)
+            HQ(0, 7)
+            NT(0, 1)
+            NT(0, 0)
+            VH(0, 6)
+            NQ(1)
+            PG(1, 6)
+            XI("S", 1, 0)
+            XQ(1, 0)
+            VH(0, 5)
+            PG(1, 7)
+            PG(1, 0)
+            PD(1, 2)
+            SD(0, 1)
+            HQ(0, 6)
+            NC("S", 0, 0)
+            PG(0, 0)
+            NC("S", 0, 1)
+            VH(1, 7)
+            XI("S", 1, 1)
+            SD(1, 2)
+            PG(1, 1)
+            HQ(0, 4)
+            VH(1, 6)
+            PD(1, 3)
+            PG(1, 4)
+            XI("S", 0, 1)
+            HQ(1, 7)
+            HQ(1, 6)
+            VH(1, 0)
+            NQ(0)
+            VH(0, 0)
+            VH(1, 1)
+            XQ(1, 1)
+            PG(0, 1)
+            XQ(0, 1)
+            SD(1, 3)
+            VH(1, 4)
+            PD(0, 2)
+            PM(7)
+            SD(0, 2)
+            SS(7)
+            VH(0, 1)
+            PM(6)
+            HQ(0, 0)
+            SS(6)
+            PG(0, 3)
+            HQ(1, 4)
+            RS(7)
+            RS(6)
+            PG(1, 3)
+            FS("S", 7)
+            PG(1, 5)
+            HQ(1, 0)
+            PM(4)
+            HQ(1, 1)
+            PM(0)
+            VH(1, 3)
+            HQ(0, 5)
+            FS("S", 6)
+            SS(4)
+            SS(0)
+            VH(0, 3)
+            ST(7)
+            HQ(1, 3)
+            HQ(0, 1)
+            PG(0, 2)
+            RS(4)
+            HQ(0, 3)
+            RS(0)
+            FS("S", 4)
+            VH(1, 5)
+            PM(3)
+            PG(1, 2)
+            SS(3)
+            VH(0, 2)
+            HQ(1, 5)
+            RS(3)
+            PM(1)
+            PM(5)
+            FS("V", 0)
+            VH(1, 2)
+            HQ(0, 2)
+            SS(1)
+            HQ(1, 2)
+            FS("V", 3)
+            SS(5)
+            ST(6)
+            RS(1)
+            RS(5)
+            FS("V", 1)
+            PM(2)
+            ST(4)
+            FS("V", 5)
+            SS(2)
+            ST(0)
+            RS(2)
+            ST(3)
+            FS("V", 2)
+            ST(1)
+            ST(5)
+            ST(2)

@@ -21,7 +21,7 @@ PACK = 4
 KP = P * PACK
 NB = DI // P
 HC = 512
-XC = ((0, 256), (256, 256), (512, 512))
+XC = ((0, 512), (512, 512))
 
 
 def tile_floramomentumsubspacetransfer_kernel(tc, m, a_old, a_new, x_bytes, x_scale, dy, out):
@@ -39,8 +39,8 @@ def tile_floramomentumsubspacetransfer_kernel(tc, m, a_old, a_new, x_bytes, x_sc
         warm = keep.tile([P, 1], F32, name="warm")
         xsc = keep.tile([P, 2, PACK], F32, name="xsc")
         xb = [keep.tile([P, PACK, DI], U8, name="xb%d" % p) for p in range(2)]
-        dyr = {(p, g): keep.tile([P, PACK, HC], BF16, name="dyr%d%d" % (p, g)) for p in range(2) for g in range(2)}
-        aor = [keep.tile([P, PACK, HC], BF16, name="aor%d" % g) for g in range(2)]
+        dyr = [keep.tile([P, PACK, DO], BF16, name="dyr%d" % p) for p in range(2)]
+        aor = keep.tile([P, PACK, DO], BF16, name="aor")
         mr = [keep.tile([P, 4, R], BF16, name="mr%d" % h) for h in range(2)]
         anr = keep.tile([P, 4, DO], BF16, name="anr")
 
@@ -55,27 +55,24 @@ def tile_floramomentumsubspacetransfer_kernel(tc, m, a_old, a_new, x_bytes, x_sc
         hq = {}
 
         nc.sync.dma_start(out=xsc[:], in_=x_scale.rearrange("(g p t) o -> p g (t o)", p=P, t=PACK))
-        for p in range(2):
-            nc.sync.dma_start(out=xb[p][:], in_=x_bytes.rearrange("(g p t) n -> g p t n", p=P, t=PACK)[p])
 
-        def load_dy(p, g):
-            nc.sync.dma_start(out=dyr[p, g][:], in_=dy.rearrange("(q p t) n -> q p t n", p=P, t=PACK)[p][:, :, g * HC : (g + 1) * HC])
+        def load_dy(p):
+            nc.sync.dma_start(out=dyr[p][:], in_=dy.rearrange("(q p t) n -> q p t n", p=P, t=PACK)[p])
 
-        def load_ao(g):
-            nc.sync.dma_start(out=aor[g][:], in_=a_old.rearrange("(p t) n -> p t n", t=PACK)[:, :, g * HC : (g + 1) * HC])
+        def load_ao():
+            nc.sync.dma_start(out=aor[:], in_=a_old.rearrange("(p t) n -> p t n", t=PACK))
 
         def load_m(h):
             nc.sync.dma_start(out=mr[h][:], in_=m.rearrange("(h i p) k -> h p i k", p=P, i=4)[h])
 
-        load_m(1)
-        load_ao(1)
-        load_ao(0)
+        nc.sync.dma_start(out=xb[1][:], in_=x_bytes.rearrange("(g p t) n -> g p t n", p=P, t=PACK)[1])
+        nc.sync.dma_start(out=xb[0][:], in_=x_bytes.rearrange("(g p t) n -> g p t n", p=P, t=PACK)[0])
+        load_ao()
         load_m(0)
-        load_dy(0, 0)
-        load_dy(1, 0)
-        load_dy(1, 1)
+        load_dy(0)
+        load_dy(1)
+        load_m(1)
         nc.sync.dma_start(out=anr[:], in_=a_new.rearrange("(i p) k -> p i k", p=P))
-        load_dy(0, 1)
 
         make_identity(nc, ident[:])
         make_identity(nc, identb[:])
@@ -93,7 +90,7 @@ def tile_floramomentumsubspacetransfer_kernel(tc, m, a_old, a_new, x_bytes, x_sc
         def XW(eng, p, c, j):
             c0, w = XC[c]
             if (p, c) not in xw:
-                xw[p, c] = wide.tile([P, PACK, w], BF16, name="xw%d" % w, bufs=1024 // w)
+                xw[p, c] = wide.tile([P, PACK, w], BF16, name="xw%d" % w, bufs=4)
             src = xb[p][:, j, c0 : c0 + w].bitcast(FP8)
             dst = xw[p, c][:, j, :]
             if eng == "S":
@@ -108,18 +105,18 @@ def tile_floramomentumsubspacetransfer_kernel(tc, m, a_old, a_new, x_bytes, x_sc
                 nc.vector.tensor_copy(out=dst, in_=src)
 
         def XI(eng, p, c):
-            xg[p, c] = group.tile([P, XC[c][1], PACK], BF16, align_bytes=64, name="xg%d" % XC[c][1], bufs=1024 // XC[c][1])
+            xg[p, c] = group.tile([P, XC[c][1], PACK], BF16, align_bytes=64, name="xg%d" % XC[c][1], bufs=4)
             copy(eng, xg[p, c][:], xw[p, c][:].rearrange("p j c -> p c j"))
 
         def XQ(p, c):
             q((xq[p, c][0][:], xq[p, c][1][:]), xg[p, c][:].rearrange("p c j -> p (c j)"))
 
         def perm(eng, dst, src):
-            copy(eng, dst[:].rearrange("p (t m) j -> p t m j", t=PACK), src[:].rearrange("p j (m t) -> p t m j", t=PACK))
+            copy(eng, dst[:].rearrange("p (t m) j -> p t m j", t=PACK), src.rearrange("p j (m t) -> p t m j", t=PACK))
 
         def DG(eng, p, g):
             dg[p, g] = group.tile([P, HC, PACK], BF16, align_bytes=64, name="grp")
-            perm(eng, dg[p, g], dyr[p, g])
+            perm(eng, dg[p, g], dyr[p][:, :, g * HC : (g + 1) * HC])
 
         def II(src, k):
             bank = psum.tile([P, 2, P, PACK], BF16, name="tr")
@@ -131,7 +128,7 @@ def tile_floramomentumsubspacetransfer_kernel(tc, m, a_old, a_new, x_bytes, x_sc
             copy(eng, dst[:, 256 * k : 256 * (k + 1), :], bank[:].rearrange("p t m j -> p (t m) j"))
 
         def DI_(p, g, k):
-            tr["d", p, g, k] = II(dyr[p, g], k)
+            tr["d", p, g, k] = II(dyr[p][:, :, g * HC : (g + 1) * HC], k)
 
         def DC(eng, p, g, k):
             if (p, g) not in dg:
@@ -139,7 +136,7 @@ def tile_floramomentumsubspacetransfer_kernel(tc, m, a_old, a_new, x_bytes, x_sc
             IC(eng, dg[p, g], tr["d", p, g, k], k)
 
         def AI(g, k):
-            tr["a", g, k] = II(aor[g], k)
+            tr["a", g, k] = II(aor[:, :, g * HC : (g + 1) * HC], k)
 
         def AC(eng, g, k):
             if g not in ag:
@@ -151,7 +148,7 @@ def tile_floramomentumsubspacetransfer_kernel(tc, m, a_old, a_new, x_bytes, x_sc
 
         def AG(eng, g):
             ag[g] = group.tile([P, HC, PACK], BF16, align_bytes=64, name="grp")
-            perm(eng, ag[g], aor[g])
+            perm(eng, ag[g], aor[:, :, g * HC : (g + 1) * HC])
 
         def AQ(g):
             q((aq[g][0][:], aq[g][1][:]), ag[g][:].rearrange("p c j -> p (c j)"))
@@ -249,202 +246,181 @@ def tile_floramomentumsubspacetransfer_kernel(tc, m, a_old, a_new, x_bytes, x_sc
             nc.sync.dma_start(out=out[P * i : P * (i + 1), :], in_=res[i][:])
 
         with tc.manual_schedule():
-            XW("V", 0, 1, 0)
-            XW("V", 0, 0, 0)
-            XW("V", 0, 2, 3)
-            XW("V", 0, 2, 1)
-            XW("V", 0, 1, 3)
-            XW("S", 0, 2, 0)
-            XW("V", 0, 0, 2)
-            XW("S", 0, 2, 2)
-            MT(1, 1)
-            MT(1, 0)
-            XW("S", 0, 0, 1)
-            XI("V", 0, 2)
-            XW("S", 0, 0, 3)
-            XW("S", 0, 1, 1)
-            AG("V", 1)
-            MC("S", 1, 1)
-            AI(0, 1)
-            MC("S", 1, 0)
-            AI(0, 0)
-            XI("S", 0, 0)
-            MQ(1, 0)
-            AQ(1)
-            MQ(1, 1)
-            XW("S", 0, 1, 2)
-            AC("S", 0, 1)
-            XQ(0, 2)
-            XQ(0, 0)
-            AC("S", 0, 0)
-            PD(1, 4)
-            AQ(0)
-            PD(1, 6)
-            XW("V", 1, 0, 2)
-            XW("V", 1, 2, 2)
-            MT(0, 0)
-            MT(0, 1)
-            SD(1, 4)
-            XW("S", 1, 0, 1)
-            MC("S", 0, 0)
-            SD(1, 6)
-            XW("V", 1, 2, 0)
-            XW("V", 1, 1, 1)
-            XW("V", 1, 1, 2)
-            MC("S", 0, 1)
-            PD(0, 6)
-            SD(0, 6)
-            XW("V", 1, 0, 0)
-            MQ(0, 0)
-            XW("V", 1, 2, 3)
-            PD(0, 5)
-            XW("V", 1, 2, 1)
-            XW("V", 1, 0, 3)
             XW("V", 1, 1, 3)
-            XI("V", 1, 2)
-            DI_(0, 0, 1)
-            MQ(0, 1)
-            PD(1, 5)
-            DI_(0, 0, 0)
-            DC("S", 0, 0, 1)
-            PD(0, 4)
-            PD(1, 1)
-            DC("S", 0, 0, 0)
-            SD(1, 5)
-            SD(0, 5)
-            PD(0, 7)
-            SD(0, 4)
-            DI_(1, 0, 0)
-            DI_(1, 0, 1)
-            PD(0, 3)
-            DC("S", 1, 0, 0)
-            DC("S", 1, 0, 1)
-            SD(1, 1)
-            XQ(1, 2)
-            PD(0, 0)
-            PD(1, 0)
-            DQ(0, 0)
-            DG("V", 1, 1)
-            PD(1, 7)
-            DQ(1, 0)
-            SD(0, 7)
-            SD(0, 3)
-            NT(1, 1)
-            DQ(1, 1)
-            NT(1, 0)
-            PG(0, 4)
-            DG("V", 0, 1)
-            PG(0, 7)
-            PG(0, 6)
-            VH(0, 7)
-            SD(0, 0)
-            PG(0, 5)
+            XW("S", 1, 0, 1)
+            XW("S", 1, 0, 0)
+            XW("V", 1, 0, 2)
+            XW("V", 1, 0, 3)
             XW("V", 1, 1, 0)
-            DQ(0, 1)
-            VH(0, 4)
-            SD(1, 0)
-            NC("S", 1, 1)
-            NC("S", 1, 0)
-            PD(0, 1)
-            SD(1, 7)
-            HQ(0, 7)
-            NT(0, 1)
-            NT(0, 0)
-            VH(0, 6)
-            NQ(1)
-            PG(1, 6)
-            XI("S", 1, 0)
+            XW("V", 0, 0, 3)
+            XW("S", 0, 0, 1)
+            XI("V", 1, 0)
+            XW("S", 0, 1, 3)
+            XW("V", 0, 0, 0)
             XQ(1, 0)
-            VH(0, 5)
-            PG(1, 7)
-            PG(1, 0)
+            XW("S", 0, 0, 2)
+            AG("V", 1)
+            MT(0, 1)
+            AG("V", 0)
+            XW("S", 0, 1, 0)
+            MT(0, 0)
+            XI("S", 0, 0)
+            AQ(1)
+            MC("S", 0, 1)
+            MQ(0, 1)
+            MC("S", 0, 0)
+            XW("S", 0, 1, 1)
+            AQ(0)
             PD(1, 2)
-            SD(0, 1)
-            HQ(0, 6)
-            NC("S", 0, 0)
-            PG(0, 0)
-            NC("S", 0, 1)
-            VH(1, 7)
-            XI("S", 1, 1)
-            SD(1, 2)
-            PG(1, 1)
-            HQ(0, 4)
-            VH(1, 6)
+            MQ(0, 0)
             PD(1, 3)
-            PG(1, 4)
-            XI("S", 0, 1)
-            HQ(1, 7)
-            HQ(1, 6)
-            VH(1, 0)
-            NQ(0)
-            VH(0, 0)
-            VH(1, 1)
-            XQ(1, 1)
-            PG(0, 1)
-            XQ(0, 1)
+            XQ(0, 0)
+            DG("V", 0, 0)
+            DG("S", 0, 1)
+            SD(1, 2)
+            PD(0, 0)
+            PD(0, 3)
+            DG("V", 1, 1)
+            PD(0, 1)
             SD(1, 3)
-            VH(1, 4)
+            PD(1, 0)
+            SD(0, 3)
+            SD(0, 0)
             PD(0, 2)
-            PM(7)
-            SD(0, 2)
-            SS(7)
-            VH(0, 1)
-            PM(6)
-            HQ(0, 0)
-            SS(6)
-            PG(0, 3)
-            HQ(1, 4)
-            RS(7)
-            RS(6)
-            PG(1, 3)
-            FS("S", 7)
-            PG(1, 5)
-            HQ(1, 0)
-            PM(4)
-            HQ(1, 1)
-            PM(0)
-            VH(1, 3)
-            HQ(0, 5)
-            FS("S", 6)
-            SS(4)
-            SS(0)
-            VH(0, 3)
-            ST(7)
-            HQ(1, 3)
-            HQ(0, 1)
-            PG(0, 2)
-            RS(4)
-            HQ(0, 3)
-            RS(0)
-            FS("S", 4)
-            VH(1, 5)
-            PM(3)
+            PD(1, 1)
+            MT(1, 1)
+            SD(0, 1)
+            DQ(0, 1)
+            MT(1, 0)
+            DQ(1, 1)
+            DQ(0, 0)
+            XW("V", 0, 1, 2)
+            MC("S", 1, 1)
             PG(1, 2)
-            SS(3)
-            VH(0, 2)
-            HQ(1, 5)
-            RS(3)
-            PM(1)
-            PM(5)
-            FS("V", 0)
+            XW("S", 1, 1, 1)
+            MC("S", 1, 0)
+            DG("V", 1, 0)
+            PG(1, 0)
+            SD(1, 0)
+            MQ(1, 0)
+            DQ(1, 0)
+            NT(1, 0)
+            NT(0, 1)
+            PD(0, 5)
+            SD(0, 2)
+            MQ(1, 1)
+            PG(1, 1)
             VH(1, 2)
-            HQ(0, 2)
-            SS(1)
+            PG(0, 0)
+            SD(1, 1)
+            XW("S", 1, 1, 2)
+            VH(1, 0)
+            SD(0, 5)
+            VH(1, 1)
+            PG(0, 3)
+            NC("S", 0, 1)
             HQ(1, 2)
-            FS("V", 3)
-            SS(5)
-            ST(6)
-            RS(1)
-            RS(5)
-            FS("V", 1)
+            VH(0, 0)
+            NC("S", 1, 0)
+            PD(0, 7)
+            XI("V", 0, 1)
+            XI("S", 1, 1)
+            VH(0, 3)
+            PG(0, 2)
+            PD(0, 6)
+            PG(0, 1)
+            SD(0, 7)
+            NT(0, 0)
+            NT(1, 1)
+            PG(1, 3)
+            VH(0, 2)
+            SD(0, 6)
+            XQ(0, 1)
+            PD(1, 4)
+            XQ(1, 1)
+            NC("S", 1, 1)
+            VH(0, 1)
+            SD(1, 4)
+            VH(1, 3)
+            HQ(0, 0)
+            PD(1, 6)
+            PG(0, 7)
+            VH(0, 7)
+            NC("S", 0, 0)
+            PD(0, 4)
+            PD(1, 7)
+            PG(0, 6)
+            HQ(0, 2)
+            PG(1, 4)
+            NQ(0)
+            SD(1, 6)
+            HQ(1, 0)
+            SD(0, 4)
+            NQ(1)
+            PD(1, 5)
+            HQ(0, 1)
+            SD(1, 7)
+            PG(0, 4)
+            SD(1, 5)
+            PM(0)
+            VH(0, 6)
+            HQ(1, 3)
+            HQ(0, 3)
+            SS(0)
+            RS(0)
+            PG(1, 7)
+            FS("S", 0)
             PM(2)
-            ST(4)
-            FS("V", 5)
+            HQ(0, 7)
             SS(2)
+            VH(1, 4)
+            VH(0, 4)
+            HQ(1, 4)
+            PM(3)
+            HQ(0, 6)
             ST(0)
+            SS(3)
+            VH(1, 7)
+            HQ(1, 1)
+            PG(1, 6)
+            HQ(0, 4)
+            HQ(1, 7)
             RS(2)
+            PG(0, 5)
+            RS(3)
+            FS("S", 2)
+            PM(4)
+            VH(1, 6)
+            PM(1)
+            FS("V", 3)
+            SS(4)
+            HQ(1, 6)
             ST(3)
-            FS("V", 2)
-            ST(1)
-            ST(5)
+            PG(1, 5)
             ST(2)
+            VH(0, 5)
+            RS(4)
+            FS("V", 4)
+            ST(4)
+            SS(1)
+            VH(1, 5)
+            HQ(0, 5)
+            PM(6)
+            HQ(1, 5)
+            RS(1)
+            SS(6)
+            FS("V", 1)
+            PM(7)
+            ST(1)
+            SS(7)
+            RS(6)
+            PM(5)
+            RS(7)
+            SS(5)
+            FS("V", 6)
+            ST(6)
+            FS("V", 7)
+            RS(5)
+            ST(7)
+            FS("V", 5)
+            ST(5)

@@ -34,7 +34,6 @@ def tile_floramomentumsubspacetransfer_kernel(tc, m, a_old, a_new, x_bytes, x_sc
         psum = ctx.enter_context(tc.psum_pool(name="psum", bufs=2))
 
         ident = keep.tile([P, P], F32, name="ident")
-        identb = keep.tile([P, P], BF16, name="identb")
         eps = keep.tile([P, 1], F32, name="eps")
         warm = keep.tile([P, 1], F32, name="warm")
         xsc = keep.tile([P, 2, PACK], F32, name="xsc")
@@ -54,7 +53,7 @@ def tile_floramomentumsubspacetransfer_kernel(tc, m, a_old, a_new, x_bytes, x_sc
         nq = [operand("nq%d" % p, R) for p in range(2)]
         hq = {}
 
-        nc.sync.dma_start(out=xsc[:], in_=x_scale.rearrange("(g p t) o -> p g (t o)", p=P, t=PACK))
+        nc.scalar.dma_start(out=xsc[:], in_=x_scale.rearrange("(g p t) o -> p g (t o)", p=P, t=PACK))
 
         def load_dy(p):
             nc.sync.dma_start(out=dyr[p][:], in_=dy.rearrange("(q p t) n -> q p t n", p=P, t=PACK)[p])
@@ -70,12 +69,11 @@ def tile_floramomentumsubspacetransfer_kernel(tc, m, a_old, a_new, x_bytes, x_sc
         load_ao()
         load_m(0)
         load_dy(0)
-        load_dy(1)
         load_m(1)
         nc.sync.dma_start(out=anr[:], in_=a_new.rearrange("(i p) k -> p i k", p=P))
+        load_dy(1)
 
         make_identity(nc, ident[:])
-        make_identity(nc, identb[:])
         nc.vector.memset(warm[:], 1.0)
         nc.vector.memset(eps[:], 0.0)
         nc.vector.tensor_scalar(out=eps[:], in0=eps[:], scalar1=0.1, scalar2=None, op0=ALU.add)
@@ -106,42 +104,21 @@ def tile_floramomentumsubspacetransfer_kernel(tc, m, a_old, a_new, x_bytes, x_sc
 
         def XI(eng, p, c):
             xg[p, c] = group.tile([P, XC[c][1], PACK], BF16, align_bytes=64, name="xg%d" % XC[c][1], bufs=4)
-            copy(eng, xg[p, c][:], xw[p, c][:].rearrange("p j c -> p c j"))
+            copy(eng, xg[p, c][:].rearrange("p (c i) j -> p c j i", i=4), xw[p, c][:].rearrange("p j (c i) -> p c j i", i=4))
 
         def XQ(p, c):
             q((xq[p, c][0][:], xq[p, c][1][:]), xg[p, c][:].rearrange("p c j -> p (c j)"))
 
         def perm(eng, dst, src):
-            copy(eng, dst[:].rearrange("p (t m) j -> p t m j", t=PACK), src.rearrange("p j (m t) -> p t m j", t=PACK))
+            copy(
+                eng,
+                dst[:].rearrange("p (t n o) j -> p n t o j", t=PACK, o=2),
+                src.rearrange("p j (n o t) -> p n t o j", t=PACK, o=2),
+            )
 
         def DG(eng, p, g):
             dg[p, g] = group.tile([P, HC, PACK], BF16, align_bytes=64, name="grp")
             perm(eng, dg[p, g], dyr[p][:, :, g * HC : (g + 1) * HC])
-
-        def II(src, k):
-            bank = psum.tile([P, 2, P, PACK], BF16, name="tr")
-            for t in range(2):
-                nc.tensor.matmul(bank[:, t, :, :], identb[:], src[:, :, 2 * k + t :: 4].rearrange("p j m -> p m j"), start=True, stop=True)
-            return bank
-
-        def IC(eng, dst, bank, k):
-            copy(eng, dst[:, 256 * k : 256 * (k + 1), :], bank[:].rearrange("p t m j -> p (t m) j"))
-
-        def DI_(p, g, k):
-            tr["d", p, g, k] = II(dyr[p][:, :, g * HC : (g + 1) * HC], k)
-
-        def DC(eng, p, g, k):
-            if (p, g) not in dg:
-                dg[p, g] = group.tile([P, HC, PACK], BF16, align_bytes=64, name="grp")
-            IC(eng, dg[p, g], tr["d", p, g, k], k)
-
-        def AI(g, k):
-            tr["a", g, k] = II(aor[:, :, g * HC : (g + 1) * HC], k)
-
-        def AC(eng, g, k):
-            if g not in ag:
-                ag[g] = group.tile([P, HC, PACK], BF16, align_bytes=64, name="grp")
-            IC(eng, ag[g], tr["a", g, k], k)
 
         def DQ(p, g):
             q((dq[p, g][0][:], dq[p, g][1][:]), dg[p, g][:].rearrange("p c j -> p (c j)"))
@@ -242,185 +219,200 @@ def tile_floramomentumsubspacetransfer_kernel(tc, m, a_old, a_new, x_bytes, x_sc
             else:
                 nc.vector.tensor_scalar(out=res[i][:], in0=pm[i][:], scalar1=rst[i][:], scalar2=None, op0=ALU.mult)
 
+        def FH(i, k):
+            if k == 0:
+                res[i] = work.tile([P, R], F32, name="res", bufs=6)
+            half = slice(R // 2 * k, R // 2 * (k + 1))
+            if k == 0:
+                nc.scalar.activation(out=res[i][:, half], in_=pm[i][:, half], func=ACT.Copy, scale=rst[i][:])
+            else:
+                nc.vector.tensor_scalar(out=res[i][:, half], in0=pm[i][:, half], scalar1=rst[i][:], scalar2=None, op0=ALU.mult)
+
+        def SH(i, k):
+            half = slice(R // 2 * k, R // 2 * (k + 1))
+            nc.sync.dma_start(out=out[P * i : P * (i + 1), half], in_=res[i][:, half])
+
         def ST(i):
             nc.sync.dma_start(out=out[P * i : P * (i + 1), :], in_=res[i][:])
 
         with tc.manual_schedule():
-            XW("V", 1, 1, 3)
-            XW("S", 1, 0, 1)
-            XW("S", 1, 0, 0)
-            XW("V", 1, 0, 2)
             XW("V", 1, 0, 3)
-            XW("V", 1, 1, 0)
-            XW("V", 0, 0, 3)
-            XW("S", 0, 0, 1)
-            XI("V", 1, 0)
-            XW("S", 0, 1, 3)
-            XW("V", 0, 0, 0)
-            XQ(1, 0)
-            XW("S", 0, 0, 2)
-            AG("V", 1)
-            MT(0, 1)
-            AG("V", 0)
-            XW("S", 0, 1, 0)
-            MT(0, 0)
-            XI("S", 0, 0)
-            AQ(1)
-            MC("S", 0, 1)
-            MQ(0, 1)
-            MC("S", 0, 0)
-            XW("S", 0, 1, 1)
-            AQ(0)
-            PD(1, 2)
-            MQ(0, 0)
-            PD(1, 3)
-            XQ(0, 0)
-            DG("V", 0, 0)
-            DG("S", 0, 1)
-            SD(1, 2)
-            PD(0, 0)
-            PD(0, 3)
-            DG("V", 1, 1)
-            PD(0, 1)
-            SD(1, 3)
-            PD(1, 0)
-            SD(0, 3)
-            SD(0, 0)
-            PD(0, 2)
-            PD(1, 1)
-            MT(1, 1)
-            SD(0, 1)
-            DQ(0, 1)
-            MT(1, 0)
-            DQ(1, 1)
-            DQ(0, 0)
-            XW("V", 0, 1, 2)
-            MC("S", 1, 1)
-            PG(1, 2)
+            XW("S", 1, 0, 2)
+            XW("S", 1, 1, 3)
             XW("S", 1, 1, 1)
+            XW("V", 1, 0, 1)
+            XW("S", 0, 0, 3)
+            XW("V", 1, 0, 0)
+            XW("V", 1, 1, 0)
+            XW("S", 0, 1, 0)
+            XW("S", 0, 0, 2)
+            XW("V", 1, 1, 2)
+            MT(0, 1)
+            XW("V", 0, 0, 1)
+            XW("V", 0, 1, 3)
+            XW("V", 0, 1, 2)
+            XI("V", 1, 1)
+            XW("S", 0, 0, 0)
+            AG("V", 1)
+            XQ(1, 1)
+            AG("S", 0)
+            MC("S", 0, 1)
+            MT(0, 0)
+            AQ(1)
+            MC("S", 0, 0)
+            XI("V", 1, 0)
+            MQ(0, 1)
+            PD(1, 2)
+            AQ(0)
+            MT(1, 0)
+            DG("S", 0, 0)
+            MT(1, 1)
             MC("S", 1, 0)
-            DG("V", 1, 0)
-            PG(1, 0)
-            SD(1, 0)
-            MQ(1, 0)
-            DQ(1, 0)
-            NT(1, 0)
-            NT(0, 1)
-            PD(0, 5)
-            SD(0, 2)
-            MQ(1, 1)
-            PG(1, 1)
-            VH(1, 2)
-            PG(0, 0)
-            SD(1, 1)
-            XW("S", 1, 1, 2)
-            VH(1, 0)
-            SD(0, 5)
-            VH(1, 1)
-            PG(0, 3)
-            NC("S", 0, 1)
-            HQ(1, 2)
-            VH(0, 0)
-            NC("S", 1, 0)
-            PD(0, 7)
-            XI("V", 0, 1)
-            XI("S", 1, 1)
-            VH(0, 3)
-            PG(0, 2)
-            PD(0, 6)
-            PG(0, 1)
-            SD(0, 7)
-            NT(0, 0)
+            MC("S", 1, 1)
+            MQ(0, 0)
+            PD(1, 0)
+            SD(1, 2)
+            XQ(1, 0)
+            PD(0, 1)
+            SD(0, 1)
+            XI("V", 0, 0)
+            PD(1, 3)
+            DG("V", 0, 1)
+            PD(0, 3)
+            XQ(0, 0)
             NT(1, 1)
-            PG(1, 3)
-            VH(0, 2)
+            SD(1, 0)
+            MQ(1, 1)
+            NC("S", 1, 1)
+            NT(0, 1)
+            PD(1, 1)
+            DQ(0, 0)
+            NC("S", 0, 1)
+            SD(1, 3)
+            PD(0, 2)
+            PD(0, 0)
+            DG("V", 1, 0)
+            SD(0, 3)
+            PD(0, 7)
+            DQ(0, 1)
+            NT(0, 0)
+            PD(1, 7)
+            DQ(1, 0)
+            SD(1, 1)
+            DG("V", 1, 1)
+            SD(0, 2)
+            SD(0, 0)
+            XW("S", 0, 1, 1)
+            SD(0, 7)
+            NT(1, 0)
+            SD(1, 7)
+            PD(0, 6)
+            PG(0, 3)
+            MQ(1, 0)
+            PG(0, 1)
             SD(0, 6)
+            DQ(1, 1)
+            VH(0, 1)
+            PG(0, 0)
+            PG(0, 2)
+            XI("S", 0, 1)
+            PG(1, 0)
+            VH(0, 3)
+            VH(0, 0)
+            PG(1, 1)
+            PD(0, 4)
+            PD(0, 5)
+            VH(0, 2)
+            PG(1, 2)
+            PG(1, 3)
+            VH(1, 1)
+            SD(0, 4)
+            VH(1, 0)
+            HQ(0, 1)
+            SD(0, 5)
+            NC("S", 1, 0)
             XQ(0, 1)
             PD(1, 4)
-            XQ(1, 1)
-            NC("S", 1, 1)
-            VH(0, 1)
-            SD(1, 4)
-            VH(1, 3)
-            HQ(0, 0)
-            PD(1, 6)
-            PG(0, 7)
-            VH(0, 7)
-            NC("S", 0, 0)
-            PD(0, 4)
-            PD(1, 7)
-            PG(0, 6)
-            HQ(0, 2)
-            PG(1, 4)
-            NQ(0)
-            SD(1, 6)
+            VH(1, 2)
             HQ(1, 0)
-            SD(0, 4)
+            PD(1, 6)
+            HQ(0, 0)
+            VH(1, 3)
             NQ(1)
             PD(1, 5)
-            HQ(0, 1)
-            SD(1, 7)
-            PG(0, 4)
-            SD(1, 5)
-            PM(0)
-            VH(0, 6)
-            HQ(1, 3)
-            HQ(0, 3)
-            SS(0)
-            RS(0)
-            PG(1, 7)
-            FS("S", 0)
-            PM(2)
-            HQ(0, 7)
-            SS(2)
-            VH(1, 4)
-            VH(0, 4)
-            HQ(1, 4)
-            PM(3)
-            HQ(0, 6)
-            ST(0)
-            SS(3)
-            VH(1, 7)
+            NC("S", 0, 0)
+            NQ(0)
+            SD(1, 4)
+            SD(1, 6)
             HQ(1, 1)
-            PG(1, 6)
-            HQ(0, 4)
-            HQ(1, 7)
-            RS(2)
+            PG(1, 7)
+            VH(1, 7)
+            SD(1, 5)
+            PG(0, 7)
             PG(0, 5)
-            RS(3)
-            FS("S", 2)
-            PM(4)
-            VH(1, 6)
-            PM(1)
-            FS("V", 3)
-            SS(4)
-            HQ(1, 6)
-            ST(3)
-            PG(1, 5)
-            ST(2)
             VH(0, 5)
+            VH(0, 7)
+            HQ(1, 7)
+            PG(1, 5)
+            PM(0)
+            PM(1)
+            SS(0)
+            PG(0, 6)
+            HQ(0, 2)
+            SS(1)
+            RS(0)
+            PG(1, 4)
+            VH(1, 5)
+            HQ(0, 7)
+            HQ(0, 5)
+            HQ(0, 3)
+            RS(1)
+            PG(1, 6)
+            FS("S", 0)
+            FS("S", 1)
+            HQ(1, 5)
+            HQ(1, 3)
+            PM(7)
+            VH(0, 6)
+            PM(5)
+            SS(7)
+            SS(5)
+            PM(3)
+            VH(1, 4)
+            RS(7)
+            PG(0, 4)
+            HQ(1, 2)
+            SS(3)
+            VH(1, 6)
+            RS(5)
+            HQ(0, 6)
+            HQ(1, 4)
+            FH(7, 0)
+            ST(0)
+            HQ(1, 6)
+            PM(2)
+            VH(0, 4)
+            RS(3)
+            FH(7, 1)
+            HQ(0, 4)
+            FS("V", 5)
+            SS(2)
+            ST(1)
+            PM(6)
+            SS(6)
+            FS("V", 3)
+            RS(2)
+            SH(7, 1)
+            RS(6)
+            FS("V", 2)
+            SH(7, 0)
+            ST(5)
+            ST(3)
+            PM(4)
+            ST(2)
+            SS(4)
+            FS("V", 6)
+            ST(6)
             RS(4)
             FS("V", 4)
             ST(4)
-            SS(1)
-            VH(1, 5)
-            HQ(0, 5)
-            PM(6)
-            HQ(1, 5)
-            RS(1)
-            SS(6)
-            FS("V", 1)
-            PM(7)
-            ST(1)
-            SS(7)
-            RS(6)
-            PM(5)
-            RS(7)
-            SS(5)
-            FS("V", 6)
-            ST(6)
-            FS("V", 7)
-            RS(5)
-            ST(7)
-            FS("V", 5)
-            ST(5)

@@ -3,7 +3,10 @@ from contextlib import ExitStack
 import concourse.mybir as mybir
 from concourse.masks import make_identity
 
-DI, R, DO, S = 1024, 512, 1024, 1024
+S = 1024
+DI = 1024
+DO = 1024
+R = 512
 
 F32 = mybir.dt.float32
 BF16 = mybir.dt.bfloat16
@@ -18,401 +21,375 @@ FLOPS = 2 * (DI * R * DO + DI * S * DO + DI * DO * R)
 
 P = 128
 PACK = 4
-KP = P * PACK
-NB = DI // P
-HC = 512
-XC = ((0, 512), (512, 512))
+PASS = P * PACK
+HALF = 512
+PAIR = 256
+
+VECTOR, SCALAR = "vector", "scalar"
 
 
 def tile_floramomentumsubspacetransfer_kernel(tc, m, a_old, a_new, x_bytes, x_scale, dy, out):
     nc = tc.nc
     with ExitStack() as ctx:
-        keep = ctx.enter_context(tc.tile_pool(name="keep", bufs=1))
-        wide = ctx.enter_context(tc.tile_pool(name="wide", bufs=4))
-        group = ctx.enter_context(tc.tile_pool(name="group", bufs=10))
-        work = ctx.enter_context(tc.tile_pool(name="work", bufs=3))
-        psum = ctx.enter_context(tc.psum_pool(name="psum", bufs=2))
-
-        ident = keep.tile([P, P], F32, name="ident")
-        eps = keep.tile([P, 1], F32, name="eps")
-        warm = keep.tile([P, 1], F32, name="warm")
-        xsc = keep.tile([P, 2, PACK], F32, name="xsc")
-        xb = [keep.tile([P, PACK, DI], U8, name="xb%d" % p) for p in range(2)]
-        dyr = [keep.tile([P, PACK, DO], BF16, name="dyr%d" % p) for p in range(2)]
-        aor = keep.tile([P, PACK, DO], BF16, name="aor")
-        mr = [keep.tile([P, 4, R], BF16, name="mr%d" % h) for h in range(2)]
-        anr = keep.tile([P, 4, DO], BF16, name="anr")
+        sbuf = ctx.enter_context(tc.tile_pool(name="sbuf", bufs=1))
+        turned = ctx.enter_context(tc.psum_pool(name="turned", bufs=2))
+        sums = ctx.enter_context(tc.psum_pool(name="sums", bufs=6))
 
         def operand(name, width):
-            return (keep.tile([P, width], U32, align_bytes=64, name=name + "c"), keep.tile([P, width], U8, align_bytes=64, name=name + "s"))
+            codes = sbuf.tile([P, width], U32, align_bytes=64, name=name + "_codes")
+            scales = sbuf.tile([P, width], U8, align_bytes=64, name=name + "_scales")
+            return codes, scales
 
-        xq = {(p, c): operand("xq%d%d" % (p, c), XC[c][1]) for p in range(2) for c in range(len(XC))}
-        dq = {(p, g): operand("dq%d%d" % (p, g), HC) for p in range(2) for g in range(2)}
-        aq = [operand("aq%d" % g, HC) for g in range(2)]
-        mq = {(h, k): operand("mq%d%d" % (h, k), 256) for h in range(2) for k in range(2)}
-        nq = [operand("nq%d" % p, R) for p in range(2)]
-        hq = {}
+        def ungrouped(name):
+            return sbuf.tile([P, HALF, PACK], BF16, align_bytes=64, name=name)
 
-        nc.scalar.dma_start(out=xsc[:], in_=x_scale.rearrange("(g p t) o -> p g (t o)", p=P, t=PACK))
+        two = range(2)
+        x_scales = sbuf.tile([P, 2, PACK], F32, name="x_scales")
+        x_first = [sbuf.tile([P, 2, DI], U8, name="x_first%d" % j) for j in two]
+        x_second = sbuf.tile([P, PACK, DI], U8, name="x_second")
+        dy_rows = [sbuf.tile([P, PACK, DO], BF16, name="dy_rows%d" % p) for p in two]
+        a_old_rows = sbuf.tile([P, PACK, DO], BF16, name="a_old_rows")
+        m_rows = [sbuf.tile([P, HALF // P, R], BF16, name="m_rows%d" % h) for h in two]
+        a_new_rows = sbuf.tile([P, R // P, DO], BF16, name="a_new_rows")
 
-        def load_dy(p):
-            nc.sync.dma_start(out=dyr[p][:], in_=dy.rearrange("(q p t) n -> q p t n", p=P, t=PACK)[p])
+        x_wide = {(p, h): sbuf.tile([P, PACK, HALF], BF16, name="x_wide%d%d" % (p, h)) for p in two for h in two}
+        x_grouped = {(p, h): ungrouped("x_grouped%d%d" % (p, h)) for p in two for h in two}
+        dy_grouped = {(p, g): ungrouped("dy_grouped%d%d" % (p, g)) for p in two for g in two}
+        a_old_grouped = [ungrouped("a_old_grouped%d" % g) for g in two]
+        m_grouped = [ungrouped("m_grouped%d" % h) for h in two]
+        a_new_grouped = [ungrouped("a_new_grouped%d" % p) for p in two]
 
-        def load_ao():
-            nc.sync.dma_start(out=aor[:], in_=a_old.rearrange("(p t) n -> p t n", t=PACK))
+        x_mx = {(p, h): operand("x%d%d" % (p, h), HALF) for p in two for h in two}
+        dy_mx = {(p, g): operand("dy%d%d" % (p, g), HALF) for p in two for g in two}
+        a_old_mx = [operand("a_old%d" % g, HALF) for g in two]
+        m_mx = {(h, k): operand("m%d%d" % (h, k), PAIR) for h in two for k in two}
+        a_new_mx = [operand("a_new%d" % p, R) for p in two]
+        h_mx = {(g, i): operand("h%d%d" % (g, i), P) for g in two for i in range(DI // P)}
 
-        def load_m(h):
-            nc.sync.dma_start(out=mr[h][:], in_=m.rearrange("(h i p) k -> h p i k", p=P, i=4)[h])
+        x_bytes_by_pass = x_bytes.rearrange("(q p t) n -> q p t n", p=P, t=PACK)
+        dy_by_pass = dy.rearrange("(q p t) n -> q p t n", p=P, t=PACK)
+        m_by_half = m.rearrange("(h i p) r -> h p i r", p=P, i=HALF // P)
+        nc.scalar.dma_start(out=x_scales[:], in_=x_scale.rearrange("(q p t) o -> p q (t o)", p=P, t=PACK))
+        nc.sync.dma_start(out=x_first[0][:], in_=x_bytes_by_pass[0][:, 0 : 2, :])
+        nc.sync.dma_start(out=x_first[1][:], in_=x_bytes_by_pass[0][:, 2 : 4, :])
+        nc.sync.dma_start(out=x_second[:], in_=x_bytes_by_pass[1])
+        nc.sync.dma_start(out=a_old_rows[:], in_=a_old.rearrange("(p t) n -> p t n", t=PACK))
+        nc.sync.dma_start(out=m_rows[0][:], in_=m_by_half[0])
+        nc.sync.dma_start(out=dy_rows[0][:], in_=dy_by_pass[0])
+        nc.sync.dma_start(out=dy_rows[1][:], in_=dy_by_pass[1])
+        nc.sync.dma_start(out=m_rows[1][:], in_=m_by_half[1])
+        nc.sync.dma_start(out=a_new_rows[:], in_=a_new.rearrange("(i p) k -> p i k", p=P))
 
-        nc.sync.dma_start(out=xb[1][:], in_=x_bytes.rearrange("(g p t) n -> g p t n", p=P, t=PACK)[1])
-        nc.sync.dma_start(out=xb[0][:], in_=x_bytes.rearrange("(g p t) n -> g p t n", p=P, t=PACK)[0])
-        load_ao()
-        load_m(0)
-        load_dy(0)
-        load_m(1)
-        nc.sync.dma_start(out=anr[:], in_=a_new.rearrange("(i p) k -> p i k", p=P))
-        load_dy(1)
+        identity = sbuf.tile([P, P], F32, name="identity")
+        epsilon = sbuf.tile([P, 1], F32, name="epsilon")
+        ones = sbuf.tile([P, 1], F32, name="ones")
+        make_identity(nc, identity[:])
+        nc.vector.memset(ones[:], 1.0)
+        nc.vector.memset(epsilon[:], 0.0)
+        nc.vector.tensor_scalar(out=epsilon[:], in0=epsilon[:], scalar1=0.1, scalar2=None, op0=ALU.add)
+        nc.scalar.activation(out=ones[:], in_=ones[:], func=ACT.Abs_reciprocal_sqrt, scale=1.0)
 
-        make_identity(nc, ident[:])
-        nc.vector.memset(warm[:], 1.0)
-        nc.vector.memset(eps[:], 0.0)
-        nc.vector.tensor_scalar(out=eps[:], in0=eps[:], scalar1=0.1, scalar2=None, op0=ALU.add)
-        nc.scalar.activation(out=warm[:], in_=warm[:], func=ACT.Abs_reciprocal_sqrt, scale=1.0)
+        banks, d_kept, h_bf16, sum_sq, rms_inverse, result = {}, {}, {}, {}, {}, {}
 
-        xw, xg, dg, ag, mg, ng = {}, {}, {}, {}, {}, {}
-        tr, pd, pg, dsb, hb, pm, ssq, rst, res = {}, {}, {}, {}, {}, {}, {}, {}, {}
-
-        def q(opnd, tile):
-            nc.vector.quantize_mx(out=opnd[0].bitcast(FP8X4), scales=opnd[1], in_=tile)
-
-        def XW(eng, p, c, j):
-            c0, w = XC[c]
-            if (p, c) not in xw:
-                xw[p, c] = wide.tile([P, PACK, w], BF16, name="xw%d" % w, bufs=4)
-            src = xb[p][:, j, c0 : c0 + w].bitcast(FP8)
-            dst = xw[p, c][:, j, :]
-            if eng == "S":
-                nc.scalar.activation(out=dst, in_=src, func=ACT.Copy, scale=xsc[:, p, j : j + 1])
+        def copy(engine, out, in_):
+            if engine == SCALAR:
+                nc.scalar.copy(out=out, in_=in_)
             else:
-                nc.vector.tensor_scalar(out=dst, in0=src, scalar1=xsc[:, p, j : j + 1], scalar2=None, op0=ALU.mult)
+                nc.vector.tensor_copy(out=out, in_=in_)
 
-        def copy(eng, dst, src):
-            if eng == "S":
-                nc.scalar.copy(out=dst, in_=src)
-            else:
-                nc.vector.tensor_copy(out=dst, in_=src)
+        def quantize(operand_mx, grouped):
+            codes, scales = operand_mx
+            nc.vector.quantize_mx(out=codes[:].bitcast(FP8X4), scales=scales[:], in_=grouped.rearrange("p c t -> p (c t)"))
 
-        def XI(eng, p, c):
-            xg[p, c] = group.tile([P, XC[c][1], PACK], BF16, align_bytes=64, name="xg%d" % XC[c][1], bufs=4)
-            copy(eng, xg[p, c][:].rearrange("p (c i) j -> p c j i", i=4), xw[p, c][:].rearrange("p j (c i) -> p c j i", i=4))
-
-        def XQ(p, c):
-            q((xq[p, c][0][:], xq[p, c][1][:]), xg[p, c][:].rearrange("p c j -> p (c j)"))
-
-        def perm(eng, dst, src):
-            copy(
-                eng,
-                dst[:].rearrange("p (t n o) j -> p n t o j", t=PACK, o=2),
-                src.rearrange("p j (n o t) -> p n t o j", t=PACK, o=2),
-            )
-
-        def DG(eng, p, g):
-            dg[p, g] = group.tile([P, HC, PACK], BF16, align_bytes=64, name="grp")
-            perm(eng, dg[p, g], dyr[p][:, :, g * HC : (g + 1) * HC])
-
-        def DQ(p, g):
-            q((dq[p, g][0][:], dq[p, g][1][:]), dg[p, g][:].rearrange("p c j -> p (c j)"))
-
-        def AG(eng, g):
-            ag[g] = group.tile([P, HC, PACK], BF16, align_bytes=64, name="grp")
-            perm(eng, ag[g], aor[:, :, g * HC : (g + 1) * HC])
-
-        def AQ(g):
-            q((aq[g][0][:], aq[g][1][:]), ag[g][:].rearrange("p c j -> p (c j)"))
-
-        def transposes(bank, rows, first_word):
-            for i in range(2):
-                for u in range(2):
-                    nc.tensor.transpose(bank[:, i, u, :], rows[i][:, first_word + u : first_word + 256 : 2], ident[:])
-
-        def MT(h, k):
-            tr["m", h, k] = psum.tile([P, 2, 2, P], F32, name="tr")
-            transposes(tr["m", h, k], [mr[h][:, 2 * k + i, :].bitcast(F32) for i in range(2)], 0)
-
-        def MC(eng, h, k):
-            if h not in mg:
-                mg[h] = group.tile([P, HC, PACK], BF16, align_bytes=64, name="grp")
-            dst = mg[h][:, 256 * k : 256 * (k + 1), :].rearrange("p c j -> p (c j)").bitcast(F32).rearrange("p (i r u) -> p i r u", i=2, u=2)
-            copy(eng, dst, tr["m", h, k][:].rearrange("p i u r -> p i r u"))
-
-        def MQ(h, k):
-            q((mq[h, k][0][:], mq[h, k][1][:]), mg[h][:, 256 * k : 256 * (k + 1), :].rearrange("p c j -> p (c j)"))
-
-        def NT(p, k):
-            tr["n", p, k] = psum.tile([P, 2, 2, P], F32, name="tr")
-            transposes(tr["n", p, k], [anr[:, 2 * k + i, :].bitcast(F32) for i in range(2)], 256 * p)
-
-        def NC(eng, p, k):
-            if p not in ng:
-                ng[p] = group.tile([P, R, PACK], BF16, align_bytes=64, name="grp")
-            dst = ng[p][:, 256 * k : 256 * (k + 1), :].rearrange("p c j -> p (c j)").bitcast(F32).rearrange("p (i r u) -> p i r u", i=2, u=2)
-            copy(eng, dst, tr["n", p, k][:].rearrange("p i u r -> p i r u"))
-
-        def NQ(p):
-            q((nq[p][0][:], nq[p][1][:]), ng[p][:].rearrange("p c j -> p (c j)"))
-
-        def mm(dst, w, wc, mov, mc, start, stop):
+        def multiply(out, stationary, stationary_columns, moving, moving_columns, start, stop):
             nc.tensor.matmul_mx(
-                out=dst,
-                lhsT=w[0][:, wc].bitcast(FP8X4),
-                lhsT_scale=w[1][:, wc],
-                rhs=mov[0][:, mc].bitcast(FP8X4),
-                rhs_scale=mov[1][:, mc],
+                out=out,
+                lhsT=stationary[0][:, stationary_columns].bitcast(FP8X4),
+                lhsT_scale=stationary[1][:, stationary_columns],
+                rhs=moving[0][:, moving_columns].bitcast(FP8X4),
+                rhs_scale=moving[1][:, moving_columns],
                 start=start,
                 stop=stop,
             )
 
-        def PG(g, i):
-            pg[g, i] = psum.tile([P, PACK, P], F32, name="acc", bufs=6)
-            c = max(c for c in range(len(XC)) if XC[c][0] <= P * i)
-            cols = slice(P * i - XC[c][0], P * i - XC[c][0] + P)
-            for t in range(PACK):
-                for p in range(2):
-                    mm(pg[g, i][:, t, :], dq[p, g], slice(P * t, P * t + P), xq[p, c], cols, p == 0, p == 1)
-
-        def PD(g, i):
-            pd[g, i] = psum.tile([P, PACK, P], F32, name="acc", bufs=6)
-            k, c = divmod(i, 2)
-            for t in range(PACK):
-                mm(pd[g, i][:, t, :], aq[g], slice(P * t, P * t + P), mq[k // 2, k % 2], slice(P * c, P * c + P), True, True)
-
-        def SD(g, i):
-            dsb[g, i] = work.tile([P, P, PACK], F32, name="dsb", bufs=16)
-            nc.scalar.activation(out=dsb[g, i][:], in_=pd[g, i][:].rearrange("p t n -> p n t"), func=ACT.Copy, scale=0.8)
-
-        def VH(g, i):
-            hb[g, i] = work.tile([P, P, PACK], BF16, align_bytes=64, name="hb", bufs=14)
-            nc.vector.scalar_tensor_tensor(out=hb[g, i][:], in0=pg[g, i][:].rearrange("p t n -> p n t"), scalar=0.6 / 32.0, in1=dsb[g, i][:], op0=ALU.mult, op1=ALU.add)
-
-        def HQ(g, i):
-            hq[g, i] = operand("h%d%d" % (g, i), P)
-            q((hq[g, i][0][:], hq[g, i][1][:]), hb[g, i][:].rearrange("p n t -> p (n t)"))
-
-        def PM(i):
-            pm[i] = psum.tile([P, R], F32, name="acc", bufs=6)
-            for g in range(2):
-                mm(pm[i][:], hq[g, i], slice(0, P), nq[g], slice(0, R), g == 0, g == 1)
-
-        def SS(i):
-            ssq[i] = work.tile([P, 1], F32, name="ssq", bufs=8)
-            rst[i] = work.tile([P, 1], F32, name="rst", bufs=8)
-            junk = work.tile([P, R], BF16, name="junk", bufs=2)
-            nc.scalar.activation(out=junk[:], in_=pm[i][:], func=ACT.Square, accum_out=ssq[i][:])
-
-        def RS(i):
-            nc.scalar.activation(out=rst[i][:], in_=ssq[i][:], func=ACT.Abs_reciprocal_sqrt, scale=1.0 / R, bias=eps[:])
-
-        def FS(eng, i):
-            res[i] = work.tile([P, R], F32, name="res", bufs=6)
-            if eng == "S":
-                nc.scalar.activation(out=res[i][:], in_=pm[i][:], func=ACT.Copy, scale=rst[i][:])
+        def widen_x(engine, p, h, t):
+            rows = x_first[t // 2][:, t % 2, :] if p == 0 else x_second[:, t, :]
+            plane = rows[:, HALF * h : HALF * (h + 1)].bitcast(FP8)
+            scale = x_scales[:, p, t : t + 1]
+            if engine == SCALAR:
+                nc.scalar.activation(out=x_wide[p, h][:, t, :], in_=plane, func=ACT.Copy, scale=scale)
             else:
-                nc.vector.tensor_scalar(out=res[i][:], in0=pm[i][:], scalar1=rst[i][:], scalar2=None, op0=ALU.mult)
+                nc.vector.tensor_scalar(out=x_wide[p, h][:, t, :], in0=plane, scalar1=scale, scalar2=None, op0=ALU.mult)
 
-        def FH(i, k):
-            if k == 0:
-                res[i] = work.tile([P, R], F32, name="res", bufs=6)
-            half = slice(R // 2 * k, R // 2 * (k + 1))
-            if k == 0:
-                nc.scalar.activation(out=res[i][:, half], in_=pm[i][:, half], func=ACT.Copy, scale=rst[i][:])
+        def group_x(engine, p, h):
+            copy(
+                engine,
+                x_grouped[p, h][:].rearrange("p (c i) t -> p c t i", i=4),
+                x_wide[p, h][:].rearrange("p t (c i) -> p c t i", i=4),
+            )
+
+        def quantize_x(p, h):
+            quantize(x_mx[p, h], x_grouped[p, h][:])
+
+        def group_stationary(engine, grouped, rows):
+            copy(
+                engine,
+                grouped[:].rearrange("p (f c o) t -> p c f o t", f=4, o=2),
+                rows.rearrange("p t (c o f) -> p c f o t", f=4, o=2),
+            )
+
+        def group_dy(engine, p, g):
+            group_stationary(engine, dy_grouped[p, g], dy_rows[p][:, :, HALF * g : HALF * (g + 1)])
+
+        def quantize_dy(p, g):
+            quantize(dy_mx[p, g], dy_grouped[p, g][:])
+
+        def group_a_old(engine, g):
+            group_stationary(engine, a_old_grouped[g], a_old_rows[:, :, HALF * g : HALF * (g + 1)])
+
+        def quantize_a_old(g):
+            quantize(a_old_mx[g], a_old_grouped[g][:])
+
+        def turn(key, row_tiles, first_word):
+            bank = turned.tile([P, 2, 2, P], F32, name="turned_bank")
+            for r in two:
+                for u in two:
+                    words = row_tiles[r].bitcast(F32)[:, first_word + u : first_word + PASS // 2 : 2]
+                    nc.tensor.transpose(bank[:, r, u, :], words, identity[:])
+            banks[key] = bank
+
+        def collect(engine, key, grouped, k):
+            words = grouped[:, PAIR * k : PAIR * (k + 1), :].rearrange("p c t -> p (c t)").bitcast(F32)
+            copy(engine, words.rearrange("p (r c u) -> p r c u", r=2, u=2), banks[key][:].rearrange("p r u c -> p r c u"))
+
+        def turn_m(h, k):
+            turn(("m", h, k), [m_rows[h][:, 2 * k + r, :] for r in two], 0)
+
+        def collect_m(h, k):
+            collect(SCALAR, ("m", h, k), m_grouped[h], k)
+
+        def quantize_m(h, k):
+            quantize(m_mx[h, k], m_grouped[h][:, PAIR * k : PAIR * (k + 1), :])
+
+        def turn_a_new(p, k):
+            turn(("a_new", p, k), [a_new_rows[:, 2 * k + r, :] for r in two], PASS // 2 * p)
+
+        def collect_a_new(p, k):
+            collect(SCALAR, ("a_new", p, k), a_new_grouped[p], k)
+
+        def quantize_a_new(p):
+            quantize(a_new_mx[p], a_new_grouped[p][:])
+
+        def multiply_d(g, i):
+            bank = sums.tile([P, 4, P], F32, name="sums_bank")
+            h, k, r = i // 4, i // 2 % 2, i % 2
+            for f in range(4):
+                multiply(bank[:, f, :], a_old_mx[g], slice(P * f, P * (f + 1)), m_mx[h, k], slice(P * r, P * (r + 1)), True, True)
+            banks["d", g, i] = bank
+
+        def keep_d(g, i):
+            d_kept[g, i] = sbuf.tile([P, P, 4], F32, name="d_kept%d%d" % (g, i))
+            nc.scalar.activation(out=d_kept[g, i][:], in_=banks["d", g, i][:].rearrange("p f n -> p n f"), func=ACT.Copy, scale=0.8)
+
+        def multiply_g(g, i):
+            bank = sums.tile([P, 4, P], F32, name="sums_bank")
+            h, c = i // 4, i % 4
+            for f in range(4):
+                for p in two:
+                    multiply(bank[:, f, :], dy_mx[p, g], slice(P * f, P * (f + 1)), x_mx[p, h], slice(P * c, P * (c + 1)), p == 0, p == 1)
+            banks["g", g, i] = bank
+
+        def mix_h(g, i):
+            h_bf16[g, i] = sbuf.tile([P, P, PACK], BF16, align_bytes=64, name="h_bf16%d%d" % (g, i))
+            nc.vector.scalar_tensor_tensor(
+                out=h_bf16[g, i][:],
+                in0=banks["g", g, i][:].rearrange("p f n -> p n f"),
+                scalar=0.6 / 32.0,
+                in1=d_kept[g, i][:],
+                op0=ALU.mult,
+                op1=ALU.add,
+            )
+
+        def quantize_h(g, i):
+            quantize(h_mx[g, i], h_bf16[g, i][:])
+
+        def multiply_mn(i):
+            banks["mn", i] = sums.tile([P, R], F32, name="sums_bank")
+            for g in two:
+                multiply(banks["mn", i][:], h_mx[g, i], slice(0, P), a_new_mx[g], slice(0, R), g == 0, g == 1)
+
+        def sum_squares(i):
+            sum_sq[i] = sbuf.tile([P, 1], F32, name="sum_sq%d" % i)
+            squares = sbuf.tile([P, R], BF16, name="squares%d" % (i % 2))
+            nc.scalar.activation(out=squares[:], in_=banks["mn", i][:], func=ACT.Square, accum_out=sum_sq[i][:])
+
+        def invert_rms(i):
+            rms_inverse[i] = sbuf.tile([P, 1], F32, name="rms_inverse%d" % i)
+            nc.scalar.activation(out=rms_inverse[i][:], in_=sum_sq[i][:], func=ACT.Abs_reciprocal_sqrt, scale=1.0 / R, bias=epsilon[:])
+
+        def normalise(engine, i, columns=slice(0, R)):
+            if i not in result:
+                result[i] = sbuf.tile([P, R], F32, name="result%d" % i)
+            if engine == SCALAR:
+                nc.scalar.activation(out=result[i][:, columns], in_=banks["mn", i][:, columns], func=ACT.Copy, scale=rms_inverse[i][:])
             else:
-                nc.vector.tensor_scalar(out=res[i][:, half], in0=pm[i][:, half], scalar1=rst[i][:], scalar2=None, op0=ALU.mult)
+                nc.vector.tensor_scalar(out=result[i][:, columns], in0=banks["mn", i][:, columns], scalar1=rms_inverse[i][:], scalar2=None, op0=ALU.mult)
 
-        def SH(i, k):
-            half = slice(R // 2 * k, R // 2 * (k + 1))
-            nc.sync.dma_start(out=out[P * i : P * (i + 1), half], in_=res[i][:, half])
+        def store(i, columns=slice(0, R)):
+            nc.sync.dma_start(out=out[P * i : P * (i + 1), columns], in_=result[i][:, columns])
 
-        def ST(i):
-            nc.sync.dma_start(out=out[P * i : P * (i + 1), :], in_=res[i][:])
+        left, right = slice(0, R // 2), slice(R // 2, R)
 
         with tc.manual_schedule():
-            XW("V", 1, 0, 3)
-            XW("S", 1, 0, 2)
-            XW("S", 1, 1, 3)
-            XW("S", 1, 1, 1)
-            XW("V", 1, 0, 1)
-            XW("S", 0, 0, 3)
-            XW("V", 1, 0, 0)
-            XW("V", 1, 1, 0)
-            XW("S", 0, 1, 0)
-            XW("S", 0, 0, 2)
-            XW("V", 1, 1, 2)
-            MT(0, 1)
-            XW("V", 0, 0, 1)
-            XW("V", 0, 1, 3)
-            XW("V", 0, 1, 2)
-            XI("V", 1, 1)
-            XW("S", 0, 0, 0)
-            AG("V", 1)
-            XQ(1, 1)
-            AG("S", 0)
-            MC("S", 0, 1)
-            MT(0, 0)
-            AQ(1)
-            MC("S", 0, 0)
-            XI("V", 1, 0)
-            MQ(0, 1)
-            PD(1, 2)
-            AQ(0)
-            MT(1, 0)
-            DG("S", 0, 0)
-            MT(1, 1)
-            MC("S", 1, 0)
-            MC("S", 1, 1)
-            MQ(0, 0)
-            PD(1, 0)
-            SD(1, 2)
-            XQ(1, 0)
-            PD(0, 1)
-            SD(0, 1)
-            XI("V", 0, 0)
-            PD(1, 3)
-            DG("V", 0, 1)
-            PD(0, 3)
-            XQ(0, 0)
-            NT(1, 1)
-            SD(1, 0)
-            MQ(1, 1)
-            NC("S", 1, 1)
-            NT(0, 1)
-            PD(1, 1)
-            DQ(0, 0)
-            NC("S", 0, 1)
-            SD(1, 3)
-            PD(0, 2)
-            PD(0, 0)
-            DG("V", 1, 0)
-            SD(0, 3)
-            PD(0, 7)
-            DQ(0, 1)
-            NT(0, 0)
-            PD(1, 7)
-            DQ(1, 0)
-            SD(1, 1)
-            DG("V", 1, 1)
-            SD(0, 2)
-            SD(0, 0)
-            XW("S", 0, 1, 1)
-            SD(0, 7)
-            NT(1, 0)
-            SD(1, 7)
-            PD(0, 6)
-            PG(0, 3)
-            MQ(1, 0)
-            PG(0, 1)
-            SD(0, 6)
-            DQ(1, 1)
-            VH(0, 1)
-            PG(0, 0)
-            PG(0, 2)
-            XI("S", 0, 1)
-            PG(1, 0)
-            VH(0, 3)
-            VH(0, 0)
-            PG(1, 1)
-            PD(0, 4)
-            PD(0, 5)
-            VH(0, 2)
-            PG(1, 2)
-            PG(1, 3)
-            VH(1, 1)
-            SD(0, 4)
-            VH(1, 0)
-            HQ(0, 1)
-            SD(0, 5)
-            NC("S", 1, 0)
-            XQ(0, 1)
-            PD(1, 4)
-            VH(1, 2)
-            HQ(1, 0)
-            PD(1, 6)
-            HQ(0, 0)
-            VH(1, 3)
-            NQ(1)
-            PD(1, 5)
-            NC("S", 0, 0)
-            NQ(0)
-            SD(1, 4)
-            SD(1, 6)
-            HQ(1, 1)
-            PG(1, 7)
-            VH(1, 7)
-            SD(1, 5)
-            PG(0, 7)
-            PG(0, 5)
-            VH(0, 5)
-            VH(0, 7)
-            HQ(1, 7)
-            PG(1, 5)
-            PM(0)
-            PM(1)
-            SS(0)
-            PG(0, 6)
-            HQ(0, 2)
-            SS(1)
-            RS(0)
-            PG(1, 4)
-            VH(1, 5)
-            HQ(0, 7)
-            HQ(0, 5)
-            HQ(0, 3)
-            RS(1)
-            PG(1, 6)
-            FS("S", 0)
-            FS("S", 1)
-            HQ(1, 5)
-            HQ(1, 3)
-            PM(7)
-            VH(0, 6)
-            PM(5)
-            SS(7)
-            SS(5)
-            PM(3)
-            VH(1, 4)
-            RS(7)
-            PG(0, 4)
-            HQ(1, 2)
-            SS(3)
-            VH(1, 6)
-            RS(5)
-            HQ(0, 6)
-            HQ(1, 4)
-            FH(7, 0)
-            ST(0)
-            HQ(1, 6)
-            PM(2)
-            VH(0, 4)
-            RS(3)
-            FH(7, 1)
-            HQ(0, 4)
-            FS("V", 5)
-            SS(2)
-            ST(1)
-            PM(6)
-            SS(6)
-            FS("V", 3)
-            RS(2)
-            SH(7, 1)
-            RS(6)
-            FS("V", 2)
-            SH(7, 0)
-            ST(5)
-            ST(3)
-            PM(4)
-            ST(2)
-            SS(4)
-            FS("V", 6)
-            ST(6)
-            RS(4)
-            FS("V", 4)
-            ST(4)
+            for p, h, t in ((0, 1, 0), (0, 0, 2), (0, 1, 2), (1, 0, 0), (1, 0, 3), (1, 0, 2), (1, 1, 1)):
+                widen_x(SCALAR, p, h, t)
+            for h, t in ((1, 1), (0, 0), (0, 1), (0, 3), (1, 3)):
+                widen_x(VECTOR, 0, h, t)
+            for k in two:
+                turn_m(0, k)
+            group_x(VECTOR, 0, 0)
+            widen_x(VECTOR, 1, 0, 1)
+            quantize_x(0, 0)
+            group_x(VECTOR, 1, 0)
+            group_a_old(SCALAR, 0)
+            group_a_old(VECTOR, 1)
+            for k in two:
+                collect_m(0, k)
+            quantize_x(1, 0)
+            quantize_a_old(0)
+            for t in (0, 2):
+                widen_x(SCALAR, 1, 1, t)
+            quantize_m(0, 0)
+            widen_x(VECTOR, 1, 1, 3)
+            quantize_m(0, 1)
+            quantize_a_old(1)
+            for p in two:
+                group_dy(VECTOR, p, 0)
+            for p in two:
+                quantize_dy(p, 0)
+            group_dy(VECTOR, 1, 1)
+            for g, i in ((0, 0), (0, 1), (0, 2), (0, 3), (1, 0), (1, 1)):
+                multiply_d(g, i)
+            for i in range(4):
+                keep_d(0, i)
+            for i in range(2, 4):
+                multiply_d(1, i)
+            for k in two:
+                turn_m(1, k)
+            group_dy(SCALAR, 0, 1)
+            keep_d(1, 0)
+            for i in range(3):
+                multiply_g(0, i)
+            quantize_dy(0, 1)
+            for k in two:
+                collect_m(1, k)
+            for k in two:
+                turn_a_new(0, k)
+            mix_h(0, 0)
+            quantize_dy(1, 1)
+            for i in range(1, 4):
+                keep_d(1, i)
+            for g, i in ((0, 3), (1, 0)):
+                multiply_g(g, i)
+            quantize_m(1, 0)
+            quantize_h(0, 0)
+            for i in range(1, 3):
+                mix_h(0, i)
+            for i in range(4, 6):
+                multiply_d(0, i)
+            for k in two:
+                collect_a_new(0, k)
+            quantize_m(1, 1)
+            quantize_h(0, 1)
+            multiply_g(1, 1)
+            group_x(SCALAR, 0, 1)
+            for g, i in ((0, 3), (1, 0)):
+                mix_h(g, i)
+            for i in range(6, 8):
+                multiply_d(0, i)
+            for i in range(4, 8):
+                keep_d(0, i)
+            for i in range(2, 4):
+                quantize_h(0, i)
+            multiply_g(1, 2)
+            group_x(VECTOR, 1, 1)
+            for k in two:
+                turn_a_new(1, k)
+            quantize_x(0, 1)
+            for k in two:
+                collect_a_new(1, k)
+            quantize_h(1, 0)
+            mix_h(1, 1)
+            multiply_g(1, 3)
+            quantize_x(1, 1)
+            for i in range(2, 4):
+                mix_h(1, i)
+            for i in range(4, 7):
+                multiply_d(1, i)
+            for p in two:
+                quantize_a_new(p)
+            for i in range(1, 3):
+                quantize_h(1, i)
+            for g, i in ((0, 4), (1, 4), (0, 5)):
+                multiply_g(g, i)
+            mix_h(0, 4)
+            quantize_h(1, 3)
+            for i in range(4, 7):
+                keep_d(1, i)
+            multiply_d(1, 7)
+            keep_d(1, 7)
+            for i in two:
+                multiply_mn(i)
+            for i in two:
+                sum_squares(i)
+            for i in two:
+                invert_rms(i)
+            normalise(SCALAR, 0)
+            store(0)
+            for g, i in ((1, 4), (0, 5)):
+                mix_h(g, i)
+            for g, i in ((1, 5), (0, 6)):
+                multiply_g(g, i)
+            mix_h(1, 5)
+            for g in two:
+                quantize_h(g, 4)
+            normalise(VECTOR, 1)
+            mix_h(0, 6)
+            for g, i in ((0, 5), (1, 5), (0, 6)):
+                quantize_h(g, i)
+            for i in range(2, 4):
+                multiply_mn(i)
+            for i in range(2, 4):
+                sum_squares(i)
+            for i in range(2, 4):
+                invert_rms(i)
+            normalise(SCALAR, 2)
+            multiply_g(1, 6)
+            mix_h(1, 6)
+            quantize_h(1, 6)
+            multiply_mn(4)
+            sum_squares(4)
+            normalise(SCALAR, 3)
+            invert_rms(4)
+            for g in two:
+                multiply_g(g, 7)
+            for g in two:
+                mix_h(g, 7)
+            for g in two:
+                quantize_h(g, 7)
+            for i in range(5, 8):
+                multiply_mn(i)
+            sum_squares(5)
+            invert_rms(5)
+            sum_squares(6)
+            invert_rms(6)
+            for i in range(4, 7):
+                normalise(VECTOR, i)
+            for i in range(1, 7):
+                store(i)
+            sum_squares(7)
+            invert_rms(7)
+            normalise(SCALAR, 7, left)
+            normalise(VECTOR, 7, right)
+            store(7, right)
+            store(7, left)

from contextlib import ExitStack

import concourse.mybir as mybir
from concourse.masks import make_identity

S = 1024
DI = 1024
DO = 1024
R = 512

F32 = mybir.dt.float32
BF16 = mybir.dt.bfloat16
U32 = mybir.dt.uint32
U8 = mybir.dt.uint8
FP8 = mybir.dt.float8_e4m3fn
FP8X4 = mybir.dt.float8_e4m3fn_x4
ACT = mybir.ActivationFunctionType
ALU = mybir.AluOpType

FLOPS = 2 * (DI * R * DO + DI * S * DO + DI * DO * R)

P = 128
PACK = 4
PASS = P * PACK
HALF = 512
PAIR = 256

VECTOR, SCALAR = "vector", "scalar"


def tile_floramomentumsubspacetransfer_kernel(tc, m, a_old, a_new, x_bytes, x_scale, dy, out):
    nc = tc.nc
    with ExitStack() as ctx:
        sbuf = ctx.enter_context(tc.tile_pool(name="sbuf", bufs=1))
        turned = ctx.enter_context(tc.psum_pool(name="turned", bufs=2))
        sums = ctx.enter_context(tc.psum_pool(name="sums", bufs=6))

        def operand(name, width):
            codes = sbuf.tile([P, width], U32, align_bytes=64, name=name + "_codes")
            scales = sbuf.tile([P, width], U8, align_bytes=64, name=name + "_scales")
            return codes, scales

        def ungrouped(name):
            return sbuf.tile([P, HALF, PACK], BF16, align_bytes=64, name=name)

        two = range(2)
        x_scales = sbuf.tile([P, 2, PACK], F32, name="x_scales")
        x_first = [sbuf.tile([P, 2, DI], U8, name="x_first%d" % j) for j in two]
        x_second = sbuf.tile([P, PACK, DI], U8, name="x_second")
        dy_rows = [sbuf.tile([P, PACK, DO], BF16, name="dy_rows%d" % p) for p in two]
        a_old_rows = sbuf.tile([P, PACK, DO], BF16, name="a_old_rows")
        m_rows = [sbuf.tile([P, HALF // P, R], BF16, name="m_rows%d" % h) for h in two]
        a_new_rows = sbuf.tile([P, R // P, DO], BF16, name="a_new_rows")

        x_wide = {(p, h): sbuf.tile([P, PACK, HALF], BF16, name="x_wide%d%d" % (p, h)) for p in two for h in two}
        x_grouped = {(p, h): ungrouped("x_grouped%d%d" % (p, h)) for p in two for h in two}
        dy_grouped = {(p, g): ungrouped("dy_grouped%d%d" % (p, g)) for p in two for g in two}
        a_old_grouped = [ungrouped("a_old_grouped%d" % g) for g in two]
        m_grouped = [ungrouped("m_grouped%d" % h) for h in two]
        a_new_grouped = [ungrouped("a_new_grouped%d" % p) for p in two]

        x_mx = {(p, h): operand("x%d%d" % (p, h), HALF) for p in two for h in two}
        dy_mx = {(p, g): operand("dy%d%d" % (p, g), HALF) for p in two for g in two}
        a_old_mx = [operand("a_old%d" % g, HALF) for g in two]
        m_mx = {(h, k): operand("m%d%d" % (h, k), PAIR) for h in two for k in two}
        a_new_mx = [operand("a_new%d" % p, R) for p in two]
        h_mx = {(g, i): operand("h%d%d" % (g, i), P) for g in two for i in range(DI // P)}

        x_bytes_by_pass = x_bytes.rearrange("(q p t) n -> q p t n", p=P, t=PACK)
        dy_by_pass = dy.rearrange("(q p t) n -> q p t n", p=P, t=PACK)
        m_by_half = m.rearrange("(h i p) r -> h p i r", p=P, i=HALF // P)
        nc.scalar.dma_start(out=x_scales[:], in_=x_scale.rearrange("(q p t) o -> p q (t o)", p=P, t=PACK))
        nc.sync.dma_start(out=x_first[0][:], in_=x_bytes_by_pass[0][:, 0 : 2, :])
        nc.sync.dma_start(out=x_first[1][:], in_=x_bytes_by_pass[0][:, 2 : 4, :])
        nc.sync.dma_start(out=x_second[:], in_=x_bytes_by_pass[1])
        nc.sync.dma_start(out=a_old_rows[:], in_=a_old.rearrange("(p t) n -> p t n", t=PACK))
        nc.sync.dma_start(out=m_rows[0][:], in_=m_by_half[0])
        nc.sync.dma_start(out=dy_rows[0][:], in_=dy_by_pass[0])
        nc.sync.dma_start(out=dy_rows[1][:], in_=dy_by_pass[1])
        nc.sync.dma_start(out=m_rows[1][:], in_=m_by_half[1])
        nc.sync.dma_start(out=a_new_rows[:], in_=a_new.rearrange("(i p) k -> p i k", p=P))

        identity = sbuf.tile([P, P], F32, name="identity")
        epsilon = sbuf.tile([P, 1], F32, name="epsilon")
        ones = sbuf.tile([P, 1], F32, name="ones")
        make_identity(nc, identity[:])
        nc.vector.memset(ones[:], 1.0)
        nc.vector.memset(epsilon[:], 0.0)
        nc.vector.tensor_scalar(out=epsilon[:], in0=epsilon[:], scalar1=0.1, scalar2=None, op0=ALU.add)
        nc.scalar.activation(out=ones[:], in_=ones[:], func=ACT.Abs_reciprocal_sqrt, scale=1.0)

        banks, d_kept, h_bf16, sum_sq, rms_inverse, result = {}, {}, {}, {}, {}, {}

        def copy(engine, out, in_):
            if engine == SCALAR:
                nc.scalar.copy(out=out, in_=in_)
            else:
                nc.vector.tensor_copy(out=out, in_=in_)

        def quantize(operand_mx, grouped):
            codes, scales = operand_mx
            nc.vector.quantize_mx(out=codes[:].bitcast(FP8X4), scales=scales[:], in_=grouped.rearrange("p c t -> p (c t)"))

        def multiply(out, stationary, stationary_columns, moving, moving_columns, start, stop):
            nc.tensor.matmul_mx(
                out=out,
                lhsT=stationary[0][:, stationary_columns].bitcast(FP8X4),
                lhsT_scale=stationary[1][:, stationary_columns],
                rhs=moving[0][:, moving_columns].bitcast(FP8X4),
                rhs_scale=moving[1][:, moving_columns],
                start=start,
                stop=stop,
            )

        def widen_x(engine, p, h, t):
            rows = x_first[t // 2][:, t % 2, :] if p == 0 else x_second[:, t, :]
            plane = rows[:, HALF * h : HALF * (h + 1)].bitcast(FP8)
            scale = x_scales[:, p, t : t + 1]
            if engine == SCALAR:
                nc.scalar.activation(out=x_wide[p, h][:, t, :], in_=plane, func=ACT.Copy, scale=scale)
            else:
                nc.vector.tensor_scalar(out=x_wide[p, h][:, t, :], in0=plane, scalar1=scale, scalar2=None, op0=ALU.mult)

        def group_x(engine, p, h):
            copy(
                engine,
                x_grouped[p, h][:].rearrange("p (c i) t -> p c t i", i=4),
                x_wide[p, h][:].rearrange("p t (c i) -> p c t i", i=4),
            )

        def quantize_x(p, h):
            quantize(x_mx[p, h], x_grouped[p, h][:])

        def group_stationary(engine, grouped, rows):
            copy(
                engine,
                grouped[:].rearrange("p (f c o) t -> p c f o t", f=4, o=2),
                rows.rearrange("p t (c o f) -> p c f o t", f=4, o=2),
            )

        def group_dy(engine, p, g):
            group_stationary(engine, dy_grouped[p, g], dy_rows[p][:, :, HALF * g : HALF * (g + 1)])

        def quantize_dy(p, g):
            quantize(dy_mx[p, g], dy_grouped[p, g][:])

        def group_a_old(engine, g):
            group_stationary(engine, a_old_grouped[g], a_old_rows[:, :, HALF * g : HALF * (g + 1)])

        def quantize_a_old(g):
            quantize(a_old_mx[g], a_old_grouped[g][:])

        def turn(key, row_tiles, first_word):
            bank = turned.tile([P, 2, 2, P], F32, name="turned_bank")
            for r in two:
                for u in two:
                    words = row_tiles[r].bitcast(F32)[:, first_word + u : first_word + PASS // 2 : 2]
                    nc.tensor.transpose(bank[:, r, u, :], words, identity[:])
            banks[key] = bank

        def collect(engine, key, grouped, k):
            words = grouped[:, PAIR * k : PAIR * (k + 1), :].rearrange("p c t -> p (c t)").bitcast(F32)
            copy(engine, words.rearrange("p (r c u) -> p r c u", r=2, u=2), banks[key][:].rearrange("p r u c -> p r c u"))

        def turn_m(h, k):
            turn(("m", h, k), [m_rows[h][:, 2 * k + r, :] for r in two], 0)

        def collect_m(h, k):
            collect(SCALAR, ("m", h, k), m_grouped[h], k)

        def quantize_m(h, k):
            quantize(m_mx[h, k], m_grouped[h][:, PAIR * k : PAIR * (k + 1), :])

        def turn_a_new(p, k):
            turn(("a_new", p, k), [a_new_rows[:, 2 * k + r, :] for r in two], PASS // 2 * p)

        def collect_a_new(p, k):
            collect(SCALAR, ("a_new", p, k), a_new_grouped[p], k)

        def quantize_a_new(p):
            quantize(a_new_mx[p], a_new_grouped[p][:])

        def multiply_d(g, i):
            bank = sums.tile([P, 4, P], F32, name="sums_bank")
            h, k, r = i // 4, i // 2 % 2, i % 2
            for f in range(4):
                multiply(bank[:, f, :], a_old_mx[g], slice(P * f, P * (f + 1)), m_mx[h, k], slice(P * r, P * (r + 1)), True, True)
            banks["d", g, i] = bank

        def keep_d(g, i):
            d_kept[g, i] = sbuf.tile([P, P, 4], F32, name="d_kept%d%d" % (g, i))
            nc.scalar.activation(out=d_kept[g, i][:], in_=banks["d", g, i][:].rearrange("p f n -> p n f"), func=ACT.Copy, scale=0.8)

        def multiply_g(g, i):
            bank = sums.tile([P, 4, P], F32, name="sums_bank")
            h, c = i // 4, i % 4
            for f in range(4):
                for p in two:
                    multiply(bank[:, f, :], dy_mx[p, g], slice(P * f, P * (f + 1)), x_mx[p, h], slice(P * c, P * (c + 1)), p == 0, p == 1)
            banks["g", g, i] = bank

        def mix_h(g, i):
            h_bf16[g, i] = sbuf.tile([P, P, PACK], BF16, align_bytes=64, name="h_bf16%d%d" % (g, i))
            nc.vector.scalar_tensor_tensor(
                out=h_bf16[g, i][:],
                in0=banks["g", g, i][:].rearrange("p f n -> p n f"),
                scalar=0.6 / 32.0,
                in1=d_kept[g, i][:],
                op0=ALU.mult,
                op1=ALU.add,
            )

        def quantize_h(g, i):
            quantize(h_mx[g, i], h_bf16[g, i][:])

        def multiply_mn(i):
            banks["mn", i] = sums.tile([P, R], F32, name="sums_bank")
            for g in two:
                multiply(banks["mn", i][:], h_mx[g, i], slice(0, P), a_new_mx[g], slice(0, R), g == 0, g == 1)

        def sum_squares(i):
            sum_sq[i] = sbuf.tile([P, 1], F32, name="sum_sq%d" % i)
            squares = sbuf.tile([P, R], BF16, name="squares%d" % (i % 2))
            nc.scalar.activation(out=squares[:], in_=banks["mn", i][:], func=ACT.Square, accum_out=sum_sq[i][:])

        def invert_rms(i):
            rms_inverse[i] = sbuf.tile([P, 1], F32, name="rms_inverse%d" % i)
            nc.scalar.activation(out=rms_inverse[i][:], in_=sum_sq[i][:], func=ACT.Abs_reciprocal_sqrt, scale=1.0 / R, bias=epsilon[:])

        def normalise(engine, i, columns=slice(0, R)):
            if i not in result:
                result[i] = sbuf.tile([P, R], F32, name="result%d" % i)
            if engine == SCALAR:
                nc.scalar.activation(out=result[i][:, columns], in_=banks["mn", i][:, columns], func=ACT.Copy, scale=rms_inverse[i][:])
            else:
                nc.vector.tensor_scalar(out=result[i][:, columns], in0=banks["mn", i][:, columns], scalar1=rms_inverse[i][:], scalar2=None, op0=ALU.mult)

        def store(i, columns=slice(0, R)):
            nc.sync.dma_start(out=out[P * i : P * (i + 1), columns], in_=result[i][:, columns])

        left, right = slice(0, R // 2), slice(R // 2, R)

        with tc.manual_schedule():
            for p, h, t in ((0, 1, 0), (0, 0, 2), (0, 1, 2), (1, 0, 0), (1, 0, 3), (1, 0, 2), (1, 1, 1)):
                widen_x(SCALAR, p, h, t)
            for h, t in ((1, 1), (0, 0), (0, 1), (0, 3), (1, 3)):
                widen_x(VECTOR, 0, h, t)
            for k in two:
                turn_m(0, k)
            group_x(VECTOR, 0, 0)
            widen_x(VECTOR, 1, 0, 1)
            quantize_x(0, 0)
            group_x(VECTOR, 1, 0)
            group_a_old(SCALAR, 0)
            group_a_old(VECTOR, 1)
            for k in two:
                collect_m(0, k)
            quantize_x(1, 0)
            quantize_a_old(0)
            for t in (0, 2):
                widen_x(SCALAR, 1, 1, t)
            quantize_m(0, 0)
            widen_x(VECTOR, 1, 1, 3)
            quantize_m(0, 1)
            quantize_a_old(1)
            for p in two:
                group_dy(VECTOR, p, 0)
            for p in two:
                quantize_dy(p, 0)
            group_dy(VECTOR, 1, 1)
            for g, i in ((0, 0), (0, 1), (0, 2), (0, 3), (1, 0), (1, 1)):
                multiply_d(g, i)
            for i in range(4):
                keep_d(0, i)
            for i in range(2, 4):
                multiply_d(1, i)
            for k in two:
                turn_m(1, k)
            group_dy(SCALAR, 0, 1)
            keep_d(1, 0)
            for i in range(3):
                multiply_g(0, i)
            quantize_dy(0, 1)
            for k in two:
                collect_m(1, k)
            for k in two:
                turn_a_new(0, k)
            mix_h(0, 0)
            quantize_dy(1, 1)
            for i in range(1, 4):
                keep_d(1, i)
            for g, i in ((0, 3), (1, 0)):
                multiply_g(g, i)
            quantize_m(1, 0)
            quantize_h(0, 0)
            for i in range(1, 3):
                mix_h(0, i)
            for i in range(4, 6):
                multiply_d(0, i)
            for k in two:
                collect_a_new(0, k)
            quantize_m(1, 1)
            quantize_h(0, 1)
            multiply_g(1, 1)
            group_x(SCALAR, 0, 1)
            for g, i in ((0, 3), (1, 0)):
                mix_h(g, i)
            for i in range(6, 8):
                multiply_d(0, i)
            for i in range(4, 8):
                keep_d(0, i)
            for i in range(2, 4):
                quantize_h(0, i)
            multiply_g(1, 2)
            group_x(VECTOR, 1, 1)
            for k in two:
                turn_a_new(1, k)
            quantize_x(0, 1)
            for k in two:
                collect_a_new(1, k)
            quantize_h(1, 0)
            mix_h(1, 1)
            multiply_g(1, 3)
            quantize_x(1, 1)
            for i in range(2, 4):
                mix_h(1, i)
            for i in range(4, 7):
                multiply_d(1, i)
            for p in two:
                quantize_a_new(p)
            for i in range(1, 3):
                quantize_h(1, i)
            for g, i in ((0, 4), (1, 4), (0, 5)):
                multiply_g(g, i)
            mix_h(0, 4)
            quantize_h(1, 3)
            for i in range(4, 7):
                keep_d(1, i)
            multiply_d(1, 7)
            keep_d(1, 7)
            for i in two:
                multiply_mn(i)
            for i in two:
                sum_squares(i)
            for i in two:
                invert_rms(i)
            normalise(SCALAR, 0)
            store(0)
            for g, i in ((1, 4), (0, 5)):
                mix_h(g, i)
            for g, i in ((1, 5), (0, 6)):
                multiply_g(g, i)
            mix_h(1, 5)
            for g in two:
                quantize_h(g, 4)
            normalise(VECTOR, 1)
            mix_h(0, 6)
            for g, i in ((0, 5), (1, 5), (0, 6)):
                quantize_h(g, i)
            for i in range(2, 4):
                multiply_mn(i)
            for i in range(2, 4):
                sum_squares(i)
            for i in range(2, 4):
                invert_rms(i)
            normalise(SCALAR, 2)
            multiply_g(1, 6)
            mix_h(1, 6)
            quantize_h(1, 6)
            multiply_mn(4)
            sum_squares(4)
            normalise(SCALAR, 3)
            invert_rms(4)
            for g in two:
                multiply_g(g, 7)
            for g in two:
                mix_h(g, 7)
            for g in two:
                quantize_h(g, 7)
            for i in range(5, 8):
                multiply_mn(i)
            sum_squares(5)
            invert_rms(5)
            sum_squares(6)
            invert_rms(6)
            for i in range(4, 7):
                normalise(VECTOR, i)
            for i in range(1, 7):
                store(i)
            sum_squares(7)
            invert_rms(7)
            normalise(SCALAR, 7, left)
            normalise(VECTOR, 7, right)
            store(7, right)
            store(7, left)
